import numpy as np
import ml_dtypes


def mxq(x, axis, fmt="e4m3"):
    dtype, down = {"e4m3": (ml_dtypes.float8_e4m3fn, 7), "e5m2": (ml_dtypes.float8_e5m2, 14)}[fmt]
    v = np.moveaxis(np.asarray(x, np.float32).astype(ml_dtypes.bfloat16).astype(np.float64), axis, -1)
    blocks = v.reshape(v.shape[:-1] + (-1, 32))
    amax = np.abs(blocks).max(-1, keepdims=True)
    byte = np.maximum(np.where(amax > 0, np.frexp(amax)[1] - 1 + 127, 0) - down, 1)
    scale = np.exp2(byte - 127.0)
    codes = (blocks / scale).astype(np.float32).astype(dtype).astype(np.float64)
    return np.moveaxis((codes * scale).reshape(v.shape), -1, axis)


WIDE = False


def mx_kscale(k):
    if not WIDE:
        return np.ones(k)
    levels = np.array([10, -10, 5, -5, 0])
    if k % 512:
        return np.exp2(np.random.permutation(np.resize(levels, k // 32))).repeat(32)
    a = np.empty((k // 512, 16))
    for p in range(k // 512):
        a[p, :8] = np.random.permutation(np.resize(levels, 8))
        for g in range(8):
            far = levels[np.abs(levels - a[p, g]) >= 10]
            a[p, g + 8] = far[np.random.randint(len(far))]
    return np.exp2(a.ravel()).repeat(32)


BF16 = ml_dtypes.bfloat16


def bf(x):
    return np.asarray(x, np.float32).astype(BF16)


def f64(x):
    return np.asarray(x).astype(np.float64)


E2M1 = np.array([0.0, 0.5, 1.0, 1.5, 2.0, 3.0, 4.0, 6.0, -0.0, -0.5, -1.0, -1.5, -2.0, -3.0, -4.0, -6.0])


def pack_weight(w, fmt):
    k, n = w.shape
    w = f64(bf(w)).reshape(k // 32, 32, n)
    amax = np.abs(w).max(1)
    if fmt == "e4m3":
        byte = np.frexp(amax)[1] - 1 + 127 - 7
    else:
        mant, ex = np.frexp(amax / 6.0)
        byte = np.where(mant > 0.5, ex, ex - 1) + 127
    byte = np.clip(np.where(amax > 0, byte, 1), 1, 254)
    scaled = (w * np.exp2(127.0 - byte)[:, None, :]).reshape(k, n).astype(np.float32)
    by_word = np.ascontiguousarray(scaled.reshape(k // 512, 128, 4, n).transpose(0, 1, 3, 2))
    if fmt == "e4m3":
        words = by_word.astype(ml_dtypes.float8_e4m3fn).view(np.uint8)
    else:
        c = by_word.astype(ml_dtypes.float4_e2m1fn).view(np.uint8) & 0xF
        words = c[..., 0::2] | (c[..., 1::2] << 4)
    return np.ascontiguousarray(words), np.ascontiguousarray(byte.astype(np.uint8).reshape(k // 512, 16, n))


def unpack_weight(words, scales, fmt):
    g, p, n, _ = words.shape
    if fmt == "e4m3":
        vals = np.ascontiguousarray(words).view(ml_dtypes.float8_e4m3fn).astype(np.float64)
    else:
        nib = np.empty((g, p, n, 4), np.uint8)
        nib[..., 0::2] = words & 0xF
        nib[..., 1::2] = words >> 4
        vals = E2M1[nib]
    vals = vals * np.repeat(np.exp2(scales.astype(np.float64) - 127.0), 8, axis=1)[..., None]
    return vals.transpose(0, 1, 3, 2).reshape(g * 512, n)
def pack4(w):
    words, scales = pack_weight(w, "e2m1")
    return words.reshape(words.shape[0], 128, -1), scales


def unpack4(words, scales):
    return unpack_weight(words.reshape(words.shape[0], 128, -1, 2), scales, "e2m1")


def planes(Y):
    n, m = Y.shape
    b = f64(bf(Y)).reshape(n // 32, 32, m)
    amax = np.abs(b).max(1)
    byte = np.clip(np.where(amax > 0, np.frexp(amax)[1] - 1 + 127 - 7, 1), 1, 254)
    codes = (b * np.exp2(127.0 - byte)[:, None, :]).reshape(n, m).astype(np.float32).astype(ml_dtypes.float8_e4m3fn).view(np.uint8)
    words = codes.reshape(n // 512, 128, 4, m).transpose(0, 1, 3, 2)
    return np.ascontiguousarray(words), np.ascontiguousarray(byte.astype(np.uint8).reshape(n // 512, 16, m))


G, R, K, A, F, M = 4, 512, 1024, 512, 1536, 512
V0 = 96.0

def setup_inputs():
    s, t = mx_kscale(K), mx_kscale(F)
    dalpha = np.random.randn(G, R, K) * s
    jac = np.random.randn(G, K, F) / np.sqrt(K) / s[:, None]
    mode = np.random.randn(G, F, M) / np.sqrt(F) * np.exp(0.4 * np.random.randn(G, 1, M)) / t[:, None]
    mass = np.exp(0.6 * np.random.randn(G, A))
    isqm = np.repeat(mass ** -0.5, F // A, axis=1) * t
    v = np.random.uniform(0.5, 3.0, (G, M))
    kt = np.random.uniform(0.7, 1.3, (G, 1))
    vfac = (1.0 - v / V0) ** 4 / v
    occ = 1.0 / (np.exp(v / kt) - 1.0)
    jac_words, jac_scales = pack4(jac.reshape(G * K, F))
    mode_words, mode_scales = pack4(mode.reshape(G * F, M))
    return {"dalpha": bf(dalpha), "jac_words": jac_words, "jac_scales": jac_scales,
            "isqm": bf(isqm), "mode_words": mode_words, "mode_scales": mode_scales,
            "vfac": bf(vfac), "occ": bf(occ)}

def reference(dalpha, jac_words, jac_scales, isqm, mode_words, mode_scales, vfac, occ):
    jac = unpack4(jac_words, jac_scales).reshape(G, K, F)
    mode = unpack4(mode_words, mode_scales).reshape(G, F, M)
    h = (mxq(f64(dalpha), 2) @ jac) * f64(isqm)[:, None, :]
    d = mxq(h, 2) @ mode
    y = d * d * f64(vfac)[:, None, :] * (1.0 + f64(occ)[:, None, :])
    Y = y.reshape(G * R, M).T
    words, scales = planes(Y)
    return y, words, scales

@@ -1,0 +1,272 @@
+from contextlib import ExitStack
+
+import concourse.mybir as mybir
+from concourse.masks import make_identity
+
+G, R, K, F, M = 4, 512, 1024, 1536, 512
+FLOPS = 2 * G * R * (K * F + F * M)
+
+F32 = mybir.dt.float32
+BF16 = mybir.dt.bfloat16
+I32 = mybir.dt.int32
+U32 = mybir.dt.uint32
+U8 = mybir.dt.uint8
+FP8X4 = mybir.dt.float8_e4m3fn_x4
+FP4X4 = mybir.dt.float4_e2m1fn_x4
+ALU = mybir.AluOpType
+ACT = mybir.ActivationFunctionType
+
+P = 128
+PASS = 512
+KP = K // PASS
+FP = F // PASS
+RT = R // P
+TILES = G * RT
+
+
+def tile_grouped_raman_intensities_k7_kernel(
+    tc, dalpha, jac_words, jac_scales, isqm, mode_words, mode_scales, vfac, occ, out_0, out_1, out_2
+):
+    nc = tc.nc
+    with ExitStack() as ctx:
+        keep = ctx.enter_context(tc.tile_pool(name="keep", bufs=1))
+        work = ctx.enter_context(tc.tile_pool(name="work", bufs=3))
+        psum = ctx.enter_context(tc.psum_pool(name="psum", bufs=1))
+        ctx.enter_context(tc.manual_schedule())
+
+        x_raw = [keep.tile([P, K], BF16, name="x_raw%d" % i, align_bytes=64) for i in range(TILES)]
+        j_words = [[keep.tile([P, KP, 2 * PASS], U8, name="j_words%d_%d" % (g, j), align_bytes=64) for j in range(FP)] for g in range(G)]
+        j_scales = [keep.tile([P, KP, F], U8, name="j_scales%d" % g, align_bytes=64) for g in range(G)]
+        l_words = [keep.tile([P, FP, 2 * M], U8, name="l_words%d" % g, align_bytes=64) for g in range(G)]
+        l_scales = [keep.tile([P, FP, M], U8, name="l_scales%d" % g, align_bytes=64) for g in range(G)]
+        isq = [keep.tile([P, F], BF16, name="isq%d" % g, align_bytes=64) for g in range(G)]
+        vf = [keep.tile([P, M], BF16, name="vf%d" % g, align_bytes=64) for g in range(G)]
+        oc = [keep.tile([P, M], BF16, name="oc%d" % g, align_bytes=64) for g in range(G)]
+        fac = [keep.tile([P, M], F32, name="fac%d" % g, align_bytes=64) for g in range(G)]
+        y_codes = [keep.tile([P, R], U32, name="y_codes%d" % g, align_bytes=64) for g in range(G)]
+        y_scales = [keep.tile([P, R], U8, name="y_scales%d" % g, align_bytes=64) for g in range(G)]
+        ident0 = keep.tile([P, P], F32, name="ident0", align_bytes=64)
+        ident = keep.tile([P, P], F32, name="ident", align_bytes=64)
+
+        out_words = out_1[0].rearrange("p m t -> p (m t)")
+
+        def load_x(i):
+            g, rt = divmod(i, RT)
+            nc.sync.dma_start(out=x_raw[i][:], in_=dalpha[g, rt * P:(rt + 1) * P, :])
+
+        def load_scales(tile, src, passes, g):
+            for q in range(4):
+                nc.sync.dma_start(
+                    out=tile[32 * q:32 * q + 4, :, :].bitcast(I32),
+                    in_=src[passes * g:passes * (g + 1), 4 * q:4 * q + 4, :].rearrange("g r n -> r g n").bitcast(I32),
+                )
+
+        def load_j(g, j):
+            nc.sync.dma_start(
+                out=j_words[g][j][:].bitcast(I32),
+                in_=jac_words[KP * g:KP * (g + 1), :, 2 * PASS * j:2 * PASS * (j + 1)].rearrange("g p n -> p g n").bitcast(I32),
+            )
+
+        def load_l(g):
+            nc.sync.dma_start(
+                out=l_words[g][:].bitcast(I32),
+                in_=mode_words[FP * g:FP * (g + 1), :, :].rearrange("g p n -> p g n").bitcast(I32),
+            )
+
+        def load_row(tile, src, g):
+            nc.sync.dma_start(out=tile[:], in_=src[g].partition_broadcast(P))
+
+        def first_stage_loads(g):
+            load_scales(j_scales[g], jac_scales, KP, g)
+            load_j(g, 0)
+            load_j(g, 1)
+            load_row(isq[g], isqm, g)
+            load_j(g, 2)
+
+        def second_stage_loads(g):
+            load_scales(l_scales[g], mode_scales, FP, g)
+            load_l(g)
+            load_row(oc[g], occ, g)
+            load_row(vf[g], vfac, g)
+
+        t = {}
+
+        def transpose_x(i):
+            bank = psum.tile([P, KP, 2, P], F32, name="ps_x", bufs=2)
+            words = x_raw[i][:].bitcast(F32)
+            for c in range(KP):
+                for u in range(2):
+                    nc.tensor.transpose(bank[:, c, u, :], words[:, 256 * c + u:256 * (c + 1):2], ident[:])
+            t["ps_x", i] = bank
+
+        def copy_x(i):
+            xg = work.tile([P, KP * PASS], BF16, name="xg", align_bytes=64)
+            nc.scalar.copy(
+                out=xg[:].bitcast(F32).rearrange("p (c r u) -> p c r u", c=KP, u=2),
+                in_=t["ps_x", i][:].rearrange("p c u r -> p c r u"),
+            )
+            t["xg", i] = xg
+
+        def quantize(name, i, src, width):
+            codes = work.tile([P, width], U32, name=name + "_codes", align_bytes=64)
+            scales = work.tile([P, width], U8, name=name + "_scales", align_bytes=64)
+            nc.vector.quantize_mx(out=codes[:].bitcast(FP8X4), scales=scales[:], in_=src)
+            t[name, i] = (codes, scales)
+
+        def stage1(i):
+            g = i // RT
+            codes, scales = t["xq", i]
+            for j in range(FP):
+                bank = psum.tile([P, PASS], F32, name="ps_h%d" % j)
+                for c in range(KP):
+                    nc.tensor.matmul_mx(
+                        out=bank[:],
+                        lhsT=codes[:, c * P:(c + 1) * P].bitcast(FP8X4),
+                        lhsT_scale=scales[:, c * P:(c + 1) * P],
+                        rhs=j_words[g][j][:, c, :].bitcast(FP4X4),
+                        rhs_scale=j_scales[g][:, c, j * PASS:(j + 1) * PASS],
+                        start=(c == 0),
+                        stop=(c == KP - 1),
+                    )
+                t["ps_h", i, j] = bank
+
+        def weight_h(i, j):
+            g = i // RT
+            hb = work.tile([P, PASS], BF16, name="hb%d" % j, align_bytes=64)
+            nc.vector.tensor_tensor(
+                out=hb[:].rearrange("r (u p e) -> r u p e", u=2, e=2),
+                in0=t["ps_h", i, j][:].rearrange("r (p u e) -> r u p e", u=2, e=2),
+                in1=isq[g][:, j * PASS:(j + 1) * PASS].rearrange("r (p u e) -> r u p e", u=2, e=2),
+                op=ALU.mult,
+            )
+            t["hb", i, j] = hb
+
+        def transpose_pair(bank, half, src):
+            words = src[:].bitcast(F32)
+            for u in range(2):
+                nc.tensor.transpose(bank[:, half, u, :], words[:, u * P:(u + 1) * P], ident[:])
+
+        def copy_turned(name, bank, lo, hi):
+            dst = work.tile([P, 2, PASS], BF16, name=name, align_bytes=64)
+            nc.scalar.copy(
+                out=dst[:, lo:hi, :].bitcast(F32).rearrange("p c (r u) -> p c r u", u=2),
+                in_=bank[:, lo:hi, :, :].rearrange("p c u r -> p c r u"),
+            )
+            return dst
+
+        def stage2(i):
+            g = i // RT
+            bank = psum.tile([P, M], F32, name="ps_d")
+            for j in range(FP):
+                codes, scales = t["hqa", i] if j < 2 else t["hqb", i]
+                c = j % 2
+                nc.tensor.matmul_mx(
+                    out=bank[:],
+                    lhsT=codes[:, c * P:(c + 1) * P].bitcast(FP8X4),
+                    lhsT_scale=scales[:, c * P:(c + 1) * P],
+                    rhs=l_words[g][:, j, :].bitcast(FP4X4),
+                    rhs_scale=l_scales[g][:, j, :],
+                    start=(j == 0),
+                    stop=(j == FP - 1),
+                )
+            t["ps_d", i] = bank
+
+        def square(i):
+            sq = work.tile([P, M], F32, name="sq", align_bytes=64)
+            nc.scalar.activation(out=sq[:], in_=t["ps_d", i][:], func=ACT.Square)
+            t["sq", i] = sq
+
+        def finish_y(i):
+            g, rt = divmod(i, RT)
+            y = work.tile([P, M], F32, name="y", align_bytes=64, bufs=4)
+            nc.vector.tensor_tensor(out=y[:], in0=t["sq", i][:], in1=fac[g][:], op=ALU.mult)
+            nc.sync.dma_start(out=out_0[g, rt * P:(rt + 1) * P, :], in_=y[:])
+            t["y", i] = y
+
+        def round_y(i):
+            yb = work.tile([P, M], BF16, name="yb", align_bytes=64)
+            nc.scalar.copy(
+                out=yb[:].rearrange("r (u p e) -> r u p e", u=2, e=2),
+                in_=t["y", i][:].rearrange("r (p u e) -> r u p e", u=2, e=2),
+            )
+            t["yb", i] = yb
+
+        def quantize_y(i, src):
+            g, rt = divmod(i, RT)
+            nc.vector.quantize_mx(
+                out=y_codes[g][:, rt * P:(rt + 1) * P].bitcast(FP8X4),
+                scales=y_scales[g][:, rt * P:(rt + 1) * P],
+                in_=src,
+            )
+            if rt == RT - 1:
+                nc.sync.dma_start(out=out_words[:, 4 * R * g:4 * R * (g + 1)].bitcast(I32), in_=y_codes[g][:].bitcast(I32))
+                for q in range(4):
+                    nc.sync.dma_start(
+                        out=out_2[0, 4 * q:4 * q + 4, R * g:R * (g + 1)].bitcast(I32),
+                        in_=y_scales[g][32 * q:32 * q + 4, :].bitcast(I32),
+                    )
+
+        def live(i):
+            return 0 <= i < TILES
+
+        make_identity(nc, ident0[:])
+        nc.scalar.activation(out=ident[:], in_=ident0[:], func=ACT.Square)
+        for g in range(G):
+            nc.vector.memset(j_scales[g][:].bitcast(I32), 0)
+            nc.vector.memset(l_scales[g][:].bitcast(I32), 0)
+        load_x(0)
+        first_stage_loads(0)
+        load_x(1)
+        load_x(2)
+        second_stage_loads(0)
+        load_x(3)
+
+        for s in range(-1, TILES + 4):
+            g, rt = divmod(s, RT)
+            if live(s + 5):
+                load_x(s + 5)
+            if live(s) and g + 1 < G and rt == 0:
+                first_stage_loads(g + 1)
+            if live(s) and g + 1 < G and rt == 2:
+                second_stage_loads(g + 1)
+
+            if live(s + 1):
+                transpose_x(s + 1)
+            if live(s - 1):
+                bank_a = psum.tile([P, 2, 2, P], F32, name="ps_ta")
+                transpose_pair(bank_a, 0, t["hb", s - 1, 0])
+                transpose_pair(bank_a, 1, t["hb", s - 1, 1])
+            if live(s - 1) or live(s - 4):
+                bank_b = psum.tile([P, 2, 2, P], F32, name="ps_tb")
+            if live(s - 1):
+                transpose_pair(bank_b, 0, t["hb", s - 1, 2])
+            if live(s - 4):
+                transpose_pair(bank_b, 1, t["yb", s - 4])
+
+            if live(s - 3):
+                square(s - 3)
+                finish_y(s - 3)
+            if live(s + 1):
+                copy_x(s + 1)
+                quantize("xq", s + 1, t["xg", s + 1][:], KP * P)
+            if live(s):
+                stage1(s)
+            if live(s - 1):
+                ha = copy_turned("ha", bank_a, 0, 2)
+                quantize("hqa", s - 1, ha[:].rearrange("p c n -> p (c n)"), 2 * P)
+            if live(s - 1) or live(s - 4):
+                hy = copy_turned("hy", bank_b, 0 if live(s - 1) else 1, 2 if live(s - 4) else 1)
+            if live(s - 3):
+                round_y(s - 3)
+            if live(s):
+                for j in range(FP):
+                    weight_h(s, j)
+            if live(s - 1):
+                quantize("hqb", s - 1, hy[:, 0, :], P)
+            if live(s - 4):
+                quantize_y(s - 4, hy[:, 1, :])
+            if live(s - 2) and (s - 2) % RT == 0:
+                gd = (s - 2) // RT
+                nc.vector.scalar_tensor_tensor(out=fac[gd][:], in0=oc[gd][:], scalar=1.0, in1=vf[gd][:], op0=ALU.add, op1=ALU.mult)
+            if live(s - 2):
+                stage2(s - 2)

@@ -22,6 +22,7 @@ KP = K // PASS
 FP = F // PASS
 RT = R // P
 TILES = G * RT
+UNSORTED = 2
 
 
 def tile_grouped_raman_intensities_k7_kernel(
@@ -40,8 +41,10 @@ def tile_grouped_raman_intensities_k7_kernel(
         l_words = [keep.tile([P, FP, 2 * M], U8, name="l_words%d" % g, align_bytes=64) for g in range(G)]
         l_scales = [keep.tile([P, FP, M], U8, name="l_scales%d" % g, align_bytes=64) for g in range(G)]
         isq = [keep.tile([P, F], BF16, name="isq%d" % g, align_bytes=64) for g in range(G)]
-        vf = [keep.tile([P, M], BF16, name="vf%d" % g, align_bytes=64) for g in range(G)]
-        oc = [keep.tile([P, M], BF16, name="oc%d" % g, align_bytes=64) for g in range(G)]
+        isq_col = keep.tile([P, G, FP, 4], BF16, name="isq_col", align_bytes=64)
+        vf_col = keep.tile([P, G, 4], BF16, name="vf_col", align_bytes=64)
+        oc_col = keep.tile([P, G, 4], BF16, name="oc_col", align_bytes=64)
+        fac_col = keep.tile([P, G, 4], F32, name="fac_col", align_bytes=64)
         fac = [keep.tile([P, M], F32, name="fac%d" % g, align_bytes=64) for g in range(G)]
         y_codes = [keep.tile([P, R], U32, name="y_codes%d" % g, align_bytes=64) for g in range(G)]
         y_scales = [keep.tile([P, R], U8, name="y_scales%d" % g, align_bytes=64) for g in range(G)]
@@ -55,10 +58,10 @@ def tile_grouped_raman_intensities_k7_kernel(
             nc.sync.dma_start(out=x_raw[i][:], in_=dalpha[g, rt * P:(rt + 1) * P, :])
 
         def load_scales(tile, src, passes, g):
-            for q in range(4):
+            for r in range(4):
                 nc.sync.dma_start(
-                    out=tile[32 * q:32 * q + 4, :, :].bitcast(I32),
-                    in_=src[passes * g:passes * (g + 1), 4 * q:4 * q + 4, :].rearrange("g r n -> r g n").bitcast(I32),
+                    out=tile[r:P:32, :, :].bitcast(I32),
+                    in_=src[passes * g:passes * (g + 1), r:16:4, :].rearrange("g q n -> q g n").bitcast(I32),
                 )
 
         def load_j(g, j):
@@ -73,31 +76,48 @@ def tile_grouped_raman_intensities_k7_kernel(
                 in_=mode_words[FP * g:FP * (g + 1), :, :].rearrange("g p n -> p g n").bitcast(I32),
             )
 
-        def load_row(tile, src, g):
-            nc.sync.dma_start(out=tile[:], in_=src[g].partition_broadcast(P))
-
         def first_stage_loads(g):
             load_scales(j_scales[g], jac_scales, KP, g)
-            load_j(g, 0)
-            load_j(g, 1)
-            load_row(isq[g], isqm, g)
-            load_j(g, 2)
+            for j in range(FP):
+                load_j(g, j)
 
         def second_stage_loads(g):
             load_scales(l_scales[g], mode_scales, FP, g)
             load_l(g)
-            load_row(oc[g], occ, g)
-            load_row(vf[g], vfac, g)
 
         t = {}
 
+        def sort_x(i):
+            xs = work.tile([P, KP, 2, P], F32, name="xs", align_bytes=64)
+            nc.scalar.copy(out=xs[:], in_=x_raw[i][:].bitcast(F32).rearrange("r (c p u) -> r c u p", c=KP, u=2))
+            t["xs", i] = xs
+
         def transpose_x(i):
-            bank = psum.tile([P, KP, 2, P], F32, name="ps_x", bufs=2)
+            bank = psum.tile([P, KP, 2, P], F32, name="ps_x")
             words = x_raw[i][:].bitcast(F32)
             for c in range(KP):
                 for u in range(2):
-                    nc.tensor.transpose(bank[:, c, u, :], words[:, 256 * c + u:256 * (c + 1):2], ident[:])
+                    src = t["xs", i][:, c, u, :] if i >= UNSORTED else words[:, 256 * c + u:256 * (c + 1):2]
+                    nc.tensor.transpose(bank[:, c, u, :], src, ident[:])
             t["ps_x", i] = bank
+
+        def spread(cols, n, name="ps_s"):
+            bank = psum.tile([P, 4, P], F32, name=name)
+            for m in range(n):
+                nc.tensor.transpose(bank[:, m, :], cols[:, m:m + 1].to_broadcast([P, P]), ident[:])
+            return bank
+
+        def spread_isq(g, lo, hi, name="ps_s"):
+            return spread(isq_col[:, g, lo:hi, :].rearrange("p j t -> p (j t)").bitcast(F32), 2 * (hi - lo), name)
+
+        def copy_isq(g, lo, hi, bank):
+            nc.vector.tensor_copy(
+                out=isq[g][:, lo * PASS:hi * PASS].bitcast(F32),
+                in_=bank[:, 0:2 * (hi - lo), :].rearrange("r m p -> r (m p)"),
+            )
+
+        def copy_fac(g, bank):
+            nc.scalar.copy(out=fac[g][:].rearrange("r (p t) -> r p t", t=4), in_=bank[:].rearrange("r t p -> r p t"))
 
         def copy_x(i):
             xg = work.tile([P, KP * PASS], BF16, name="xg", align_bytes=64)
@@ -136,7 +156,7 @@ def tile_grouped_raman_intensities_k7_kernel(
             nc.vector.tensor_tensor(
                 out=hb[:].rearrange("r (u p e) -> r u p e", u=2, e=2),
                 in0=t["ps_h", i, j][:].rearrange("r (p u e) -> r u p e", u=2, e=2),
-                in1=isq[g][:, j * PASS:(j + 1) * PASS].rearrange("r (p u e) -> r u p e", u=2, e=2),
+                in1=isq[g][:, j * PASS:(j + 1) * PASS].rearrange("r (u p e) -> r u p e", u=2, e=2),
                 op=ALU.mult,
             )
             t["hb", i, j] = hb
@@ -146,17 +166,17 @@ def tile_grouped_raman_intensities_k7_kernel(
             for u in range(2):
                 nc.tensor.transpose(bank[:, half, u, :], words[:, u * P:(u + 1) * P], ident[:])
 
-        def copy_turned(name, bank, lo, hi):
+        def copy_turned(name, bank, lo, hi, move=nc.scalar.copy):
             dst = work.tile([P, 2, PASS], BF16, name=name, align_bytes=64)
-            nc.scalar.copy(
+            move(
                 out=dst[:, lo:hi, :].bitcast(F32).rearrange("p c (r u) -> p c r u", u=2),
                 in_=bank[:, lo:hi, :, :].rearrange("p c u r -> p c r u"),
             )
             return dst
 
-        def stage2(i):
+        def stage2(i, name="ps_d"):
             g = i // RT
-            bank = psum.tile([P, M], F32, name="ps_d")
+            bank = psum.tile([P, M], F32, name=name)
             for j in range(FP):
                 codes, scales = t["hqa", i] if j < 2 else t["hqb", i]
                 c = j % 2
@@ -183,9 +203,9 @@ def tile_grouped_raman_intensities_k7_kernel(
             nc.sync.dma_start(out=out_0[g, rt * P:(rt + 1) * P, :], in_=y[:])
             t["y", i] = y
 
-        def round_y(i):
+        def round_y(i, move=nc.scalar.copy):
             yb = work.tile([P, M], BF16, name="yb", align_bytes=64)
-            nc.scalar.copy(
+            move(
                 out=yb[:].rearrange("r (u p e) -> r u p e", u=2, e=2),
                 in_=t["y", i][:].rearrange("r (p u e) -> r u p e", u=2, e=2),
             )
@@ -198,13 +218,18 @@ def tile_grouped_raman_intensities_k7_kernel(
                 scales=y_scales[g][:, rt * P:(rt + 1) * P],
                 in_=src,
             )
-            if rt == RT - 1:
-                nc.sync.dma_start(out=out_words[:, 4 * R * g:4 * R * (g + 1)].bitcast(I32), in_=y_codes[g][:].bitcast(I32))
-                for q in range(4):
-                    nc.sync.dma_start(
-                        out=out_2[0, 4 * q:4 * q + 4, R * g:R * (g + 1)].bitcast(I32),
-                        in_=y_scales[g][32 * q:32 * q + 4, :].bitcast(I32),
-                    )
+
+        def store_codes(g, lo, hi):
+            nc.sync.dma_start(
+                out=out_words[:, 4 * (R * g + lo):4 * (R * g + hi)].bitcast(I32), in_=y_codes[g][:, lo:hi].bitcast(I32)
+            )
+
+        def store_scales(g, queues):
+            for q in range(4):
+                queues[q].dma_start(
+                    out=out_2[0, 4 * q:4 * q + 4, R * g:R * (g + 1)].bitcast(I32),
+                    in_=y_scales[g][32 * q:32 * q + 4, :].bitcast(I32),
+                )
 
         def live(i):
             return 0 <= i < TILES
@@ -215,33 +240,57 @@ def tile_grouped_raman_intensities_k7_kernel(
             nc.vector.memset(j_scales[g][:].bitcast(I32), 0)
             nc.vector.memset(l_scales[g][:].bitcast(I32), 0)
         load_x(0)
-        first_stage_loads(0)
+        nc.sync.dma_start(out=isq_col[:].rearrange("p g j t -> p (g j) t"), in_=isqm.rearrange("g (j p t) -> p (g j) t", p=P, t=4))
         load_x(1)
+        first_stage_loads(0)
         load_x(2)
+        nc.sync.dma_start(out=vf_col[:], in_=vfac.rearrange("g (p t) -> p g t", t=4))
+        nc.sync.dma_start(out=oc_col[:], in_=occ.rearrange("g (p t) -> p g t", t=4))
         second_stage_loads(0)
         load_x(3)
+        load_x(4)
 
-        for s in range(-1, TILES + 4):
+        transpose_x(0)
+        first_a = spread_isq(0, 0, 2)
+        first_b = spread_isq(0, 2, 3, "ps_d")
+        copy_x(0)
+        quantize("xq", 0, t["xg", 0][:], KP * P)
+        transpose_x(1)
+        copy_isq(0, 0, 2, first_a)
+        copy_isq(0, 2, 3, first_b)
+        copy_x(1)
+        stage1(0)
+        quantize("xq", 1, t["xg", 1][:], KP * P)
+        sort_x(2)
+        weight_h(0, 0)
+        weight_h(0, 1)
+        weight_h(0, 2)
+        nc.vector.scalar_tensor_tensor(out=fac_col[:], in0=oc_col[:], scalar=1.0, in1=vf_col[:], op0=ALU.add, op1=ALU.mult)
+
+        for s in range(1, TILES):
             g, rt = divmod(s, RT)
-            if live(s + 5):
-                load_x(s + 5)
-            if live(s) and g + 1 < G and rt == 0:
+            if live(s + 4):
+                load_x(s + 4)
+            if g + 1 < G and rt == 1:
                 first_stage_loads(g + 1)
-            if live(s) and g + 1 < G and rt == 2:
+            if g + 1 < G and rt == 3:
                 second_stage_loads(g + 1)
 
             if live(s + 1):
                 transpose_x(s + 1)
-            if live(s - 1):
-                bank_a = psum.tile([P, 2, 2, P], F32, name="ps_ta")
-                transpose_pair(bank_a, 0, t["hb", s - 1, 0])
-                transpose_pair(bank_a, 1, t["hb", s - 1, 1])
-            if live(s - 1) or live(s - 4):
-                bank_b = psum.tile([P, 2, 2, P], F32, name="ps_tb")
-            if live(s - 1):
-                transpose_pair(bank_b, 0, t["hb", s - 1, 2])
+            bank_a = psum.tile([P, 2, 2, P], F32, name="ps_ta")
+            transpose_pair(bank_a, 0, t["hb", s - 1, 0])
+            transpose_pair(bank_a, 1, t["hb", s - 1, 1])
+            bank_b = psum.tile([P, 2, 2, P], F32, name="ps_tb")
+            transpose_pair(bank_b, 0, t["hb", s - 1, 2])
             if live(s - 4):
                 transpose_pair(bank_b, 1, t["yb", s - 4])
+            if rt == 1:
+                bank_s = spread(fac_col[:, g, :], 4)
+            if rt == 2 and g + 1 < G:
+                bank_s = spread_isq(g + 1, 0, 2)
+            if rt == 3 and g + 1 < G:
+                bank_s = spread_isq(g + 1, 2, 3)
 
             if live(s - 3):
                 square(s - 3)
@@ -249,24 +298,76 @@ def tile_grouped_raman_intensities_k7_kernel(
             if live(s + 1):
                 copy_x(s + 1)
                 quantize("xq", s + 1, t["xg", s + 1][:], KP * P)
-            if live(s):
-                stage1(s)
-            if live(s - 1):
-                ha = copy_turned("ha", bank_a, 0, 2)
-                quantize("hqa", s - 1, ha[:].rearrange("p c n -> p (c n)"), 2 * P)
-            if live(s - 1) or live(s - 4):
-                hy = copy_turned("hy", bank_b, 0 if live(s - 1) else 1, 2 if live(s - 4) else 1)
+            stage1(s)
+            ha = copy_turned("ha", bank_a, 0, 2)
+            quantize("hqa", s - 1, ha[:].rearrange("p c n -> p (c n)"), 2 * P)
+            hy = copy_turned("hy", bank_b, 0, 2 if live(s - 4) else 1)
             if live(s - 3):
                 round_y(s - 3)
-            if live(s):
-                for j in range(FP):
-                    weight_h(s, j)
-            if live(s - 1):
-                quantize("hqb", s - 1, hy[:, 0, :], P)
+            if live(s + 2):
+                sort_x(s + 2)
+            if rt == 1:
+                copy_fac(g, bank_s)
+            for j in range(FP):
+                weight_h(s, j)
+            quantize("hqb", s - 1, hy[:, 0, :], P)
             if live(s - 4):
                 quantize_y(s - 4, hy[:, 1, :])
-            if live(s - 2) and (s - 2) % RT == 0:
-                gd = (s - 2) // RT
-                nc.vector.scalar_tensor_tensor(out=fac[gd][:], in0=oc[gd][:], scalar=1.0, in1=vf[gd][:], op0=ALU.add, op1=ALU.mult)
+                if rt == RT - 1:
+                    store_codes(g - 1, 0, R)
+                    store_scales(g - 1, [nc.sync] * 4)
+            if rt == 2 and g + 1 < G:
+                copy_isq(g + 1, 0, 2, bank_s)
+            if rt == 3 and g + 1 < G:
+                copy_isq(g + 1, 2, 3, bank_s)
             if live(s - 2):
                 stage2(s - 2)
+
+        last = TILES - 1
+        bank_a = psum.tile([P, 2, 2, P], F32, name="ps_ta")
+        transpose_pair(bank_a, 0, t["hb", last, 0])
+        transpose_pair(bank_a, 1, t["hb", last, 1])
+        bank_b = psum.tile([P, 2, 2, P], F32, name="ps_tb")
+        transpose_pair(bank_b, 0, t["hb", last, 2])
+        transpose_pair(bank_b, 1, t["yb", last - 3])
+        square(last - 2)
+        ha = copy_turned("ha", bank_a, 0, 2)
+        hy = copy_turned("hy", bank_b, 0, 2)
+        finish_y(last - 2)
+        quantize("hqa", last, ha[:].rearrange("p c n -> p (c n)"), 2 * P)
+        round_y(last - 2, nc.vector.tensor_copy)
+        stage2(last - 1, "ps_h0")
+        square(last - 1)
+        quantize("hqb", last, hy[:, 0, :], P)
+        quantize_y(last - 3, hy[:, 1, :])
+        stage2(last, "ps_h1")
+        finish_y(last - 1)
+        sq = work.tile([P, M], F32, name="sq", align_bytes=64)
+        yb = work.tile([P, M], BF16, name="yb", align_bytes=64)
+        for h in range(2):
+            cols = slice(h * M // 2, (h + 1) * M // 2)
+            nc.scalar.activation(out=sq[:, cols], in_=t["ps_d", last][:, cols], func=ACT.Square)
+            nc.vector.tensor_tensor(
+                out=yb[:].rearrange("r (u p e) -> r u p e", u=2, e=2)[:, :, h * P // 2:(h + 1) * P // 2, :],
+                in0=sq[:, cols].rearrange("r (p u e) -> r u p e", u=2, e=2),
+                in1=fac[G - 1][:, cols].rearrange("r (p u e) -> r u p e", u=2, e=2),
+                op=ALU.mult,
+            )
+        t["sq", last] = sq
+        t["yb", last] = yb
+        round_y(last - 1)
+        turned = []
+        for n, name in enumerate(["ps_ta", "ps_tb", "ps_x"]):
+            bank = psum.tile([P, 2, 2, P], F32, name=name)
+            transpose_pair(bank, 0, t["yb", last - 2 + n])
+            turned.append(bank)
+        y_a = copy_turned("ha", turned[0], 0, 1)
+        y_b = copy_turned("hy", turned[1], 0, 1)
+        finish_y(last)
+        quantize_y(last - 2, y_a[:, 0, :])
+        y_c = copy_turned("ha", turned[2], 0, 1, nc.vector.tensor_copy)
+        quantize_y(last - 1, y_b[:, 0, :])
+        store_codes(G - 1, 0, R - P)
+        quantize_y(last, y_c[:, 0, :])
+        store_codes(G - 1, R - P, R)
+        store_scales(G - 1, [nc.scalar, nc.scalar, nc.sync, nc.sync])

@@ -41,10 +41,9 @@ def tile_grouped_raman_intensities_k7_kernel(
         l_words = [keep.tile([P, FP, 2 * M], U8, name="l_words%d" % g, align_bytes=64) for g in range(G)]
         l_scales = [keep.tile([P, FP, M], U8, name="l_scales%d" % g, align_bytes=64) for g in range(G)]
         isq = [keep.tile([P, F], BF16, name="isq%d" % g, align_bytes=64) for g in range(G)]
-        isq_col = keep.tile([P, G, FP, 4], BF16, name="isq_col", align_bytes=64)
-        vf_col = keep.tile([P, G, 4], BF16, name="vf_col", align_bytes=64)
-        oc_col = keep.tile([P, G, 4], BF16, name="oc_col", align_bytes=64)
-        fac_col = keep.tile([P, G, 4], F32, name="fac_col", align_bytes=64)
+        isq_col = keep.tile([P, FP, 4], BF16, name="isq_col", align_bytes=64)
+        vf = [keep.tile([P, M], BF16, name="vf%d" % g, align_bytes=64) for g in range(G)]
+        oc = [keep.tile([P, M], BF16, name="oc%d" % g, align_bytes=64) for g in range(G)]
         fac = [keep.tile([P, M], F32, name="fac%d" % g, align_bytes=64) for g in range(G)]
         y_codes = [keep.tile([P, R], U32, name="y_codes%d" % g, align_bytes=64) for g in range(G)]
         y_scales = [keep.tile([P, R], U8, name="y_scales%d" % g, align_bytes=64) for g in range(G)]
@@ -76,14 +75,21 @@ def tile_grouped_raman_intensities_k7_kernel(
                 in_=mode_words[FP * g:FP * (g + 1), :, :].rearrange("g p n -> p g n").bitcast(I32),
             )
 
+        def load_row(tile, src, g):
+            nc.sync.dma_start(out=tile[:], in_=src[g].partition_broadcast(P))
+
         def first_stage_loads(g):
             load_scales(j_scales[g], jac_scales, KP, g)
             for j in range(FP):
                 load_j(g, j)
+            if g > 0:
+                load_row(isq[g], isqm, g)
 
         def second_stage_loads(g):
             load_scales(l_scales[g], mode_scales, FP, g)
             load_l(g)
+            load_row(oc[g], occ, g)
+            load_row(vf[g], vfac, g)
 
         t = {}
 
@@ -93,7 +99,7 @@ def tile_grouped_raman_intensities_k7_kernel(
             t["xs", i] = xs
 
         def transpose_x(i):
-            bank = psum.tile([P, KP, 2, P], F32, name="ps_x")
+            bank = psum.tile([P, KP, 2, P], F32, name="ps_x", bufs=2)
             words = x_raw[i][:].bitcast(F32)
             for c in range(KP):
                 for u in range(2):
@@ -101,23 +107,19 @@ def tile_grouped_raman_intensities_k7_kernel(
                     nc.tensor.transpose(bank[:, c, u, :], src, ident[:])
             t["ps_x", i] = bank
 
-        def spread(cols, n, name="ps_s"):
-            bank = psum.tile([P, 4, P], F32, name=name)
-            for m in range(n):
-                nc.tensor.transpose(bank[:, m, :], cols[:, m:m + 1].to_broadcast([P, P]), ident[:])
+        def spread_isq(lo, hi, name):
+            bank = psum.tile([P, 2, 2, P], F32, name=name)
+            for j in range(lo, hi):
+                words = isq_col[:, j, :].bitcast(F32)
+                for u in range(2):
+                    nc.tensor.transpose(bank[:, j - lo, u, :], words[:, u:u + 1].to_broadcast([P, P]), ident[:])
             return bank
 
-        def spread_isq(g, lo, hi, name="ps_s"):
-            return spread(isq_col[:, g, lo:hi, :].rearrange("p j t -> p (j t)").bitcast(F32), 2 * (hi - lo), name)
-
-        def copy_isq(g, lo, hi, bank):
+        def copy_isq(lo, hi, bank):
             nc.vector.tensor_copy(
-                out=isq[g][:, lo * PASS:hi * PASS].bitcast(F32),
-                in_=bank[:, 0:2 * (hi - lo), :].rearrange("r m p -> r (m p)"),
+                out=isq[0][:, lo * PASS:hi * PASS].bitcast(F32).rearrange("r (j p u) -> r j p u", p=P, u=2),
+                in_=bank[:, 0:hi - lo, :, :].rearrange("r j u p -> r j p u"),
             )
-
-        def copy_fac(g, bank):
-            nc.scalar.copy(out=fac[g][:].rearrange("r (p t) -> r p t", t=4), in_=bank[:].rearrange("r t p -> r p t"))
 
         def copy_x(i):
             xg = work.tile([P, KP * PASS], BF16, name="xg", align_bytes=64)
@@ -156,7 +158,7 @@ def tile_grouped_raman_intensities_k7_kernel(
             nc.vector.tensor_tensor(
                 out=hb[:].rearrange("r (u p e) -> r u p e", u=2, e=2),
                 in0=t["ps_h", i, j][:].rearrange("r (p u e) -> r u p e", u=2, e=2),
-                in1=isq[g][:, j * PASS:(j + 1) * PASS].rearrange("r (u p e) -> r u p e", u=2, e=2),
+                in1=isq[g][:, j * PASS:(j + 1) * PASS].rearrange("r (p u e) -> r u p e", u=2, e=2),
                 op=ALU.mult,
             )
             t["hb", i, j] = hb
@@ -196,10 +198,10 @@ def tile_grouped_raman_intensities_k7_kernel(
             nc.scalar.activation(out=sq[:], in_=t["ps_d", i][:], func=ACT.Square)
             t["sq", i] = sq
 
-        def finish_y(i):
+        def finish_y(i, engine=nc.vector):
             g, rt = divmod(i, RT)
             y = work.tile([P, M], F32, name="y", align_bytes=64, bufs=4)
-            nc.vector.tensor_tensor(out=y[:], in0=t["sq", i][:], in1=fac[g][:], op=ALU.mult)
+            engine.tensor_tensor(out=y[:], in0=t["sq", i][:], in1=fac[g][:], op=ALU.mult)
             nc.sync.dma_start(out=out_0[g, rt * P:(rt + 1) * P, :], in_=y[:])
             t["y", i] = y
 
@@ -210,6 +212,9 @@ def tile_grouped_raman_intensities_k7_kernel(
                 in_=t["y", i][:].rearrange("r (p u e) -> r u p e", u=2, e=2),
             )
             t["yb", i] = yb
+
+        def pool_cast(out, in_):
+            nc.gpsimd.tensor_scalar(out=out, in0=in_, scalar1=1.0, scalar2=0.0, op0=ALU.mult, op1=ALU.add)
 
         def quantize_y(i, src):
             g, rt = divmod(i, RT)
@@ -240,37 +245,35 @@ def tile_grouped_raman_intensities_k7_kernel(
             nc.vector.memset(j_scales[g][:].bitcast(I32), 0)
             nc.vector.memset(l_scales[g][:].bitcast(I32), 0)
         load_x(0)
-        nc.sync.dma_start(out=isq_col[:].rearrange("p g j t -> p (g j) t"), in_=isqm.rearrange("g (j p t) -> p (g j) t", p=P, t=4))
+        nc.sync.dma_start(out=isq_col[:], in_=isqm[0].rearrange("(j p t) -> p j t", p=P, t=4))
         load_x(1)
         first_stage_loads(0)
         load_x(2)
-        nc.sync.dma_start(out=vf_col[:], in_=vfac.rearrange("g (p t) -> p g t", t=4))
-        nc.sync.dma_start(out=oc_col[:], in_=occ.rearrange("g (p t) -> p g t", t=4))
-        second_stage_loads(0)
         load_x(3)
         load_x(4)
+        second_stage_loads(0)
+        load_x(5)
 
         transpose_x(0)
-        first_a = spread_isq(0, 0, 2)
-        first_b = spread_isq(0, 2, 3, "ps_d")
+        first_a = spread_isq(0, 2, "ps_ta")
+        first_b = spread_isq(2, 3, "ps_tb")
         copy_x(0)
         quantize("xq", 0, t["xg", 0][:], KP * P)
         transpose_x(1)
-        copy_isq(0, 0, 2, first_a)
-        copy_isq(0, 2, 3, first_b)
+        copy_isq(0, 2, first_a)
+        copy_isq(2, 3, first_b)
         copy_x(1)
         stage1(0)
         quantize("xq", 1, t["xg", 1][:], KP * P)
         sort_x(2)
-        weight_h(0, 0)
-        weight_h(0, 1)
-        weight_h(0, 2)
-        nc.vector.scalar_tensor_tensor(out=fac_col[:], in0=oc_col[:], scalar=1.0, in1=vf_col[:], op0=ALU.add, op1=ALU.mult)
+        sort_x(3)
+        for j in range(FP):
+            weight_h(0, j)
 
         for s in range(1, TILES):
             g, rt = divmod(s, RT)
-            if live(s + 4):
-                load_x(s + 4)
+            if live(s + 5):
+                load_x(s + 5)
             if g + 1 < G and rt == 1:
                 first_stage_loads(g + 1)
             if g + 1 < G and rt == 3:
@@ -285,41 +288,30 @@ def tile_grouped_raman_intensities_k7_kernel(
             transpose_pair(bank_b, 0, t["hb", s - 1, 2])
             if live(s - 4):
                 transpose_pair(bank_b, 1, t["yb", s - 4])
-            if rt == 1:
-                bank_s = spread(fac_col[:, g, :], 4)
-            if rt == 2 and g + 1 < G:
-                bank_s = spread_isq(g + 1, 0, 2)
-            if rt == 3 and g + 1 < G:
-                bank_s = spread_isq(g + 1, 2, 3)
 
-            if live(s - 3):
-                square(s - 3)
-                finish_y(s - 3)
             if live(s + 1):
                 copy_x(s + 1)
                 quantize("xq", s + 1, t["xg", s + 1][:], KP * P)
             stage1(s)
-            ha = copy_turned("ha", bank_a, 0, 2)
-            quantize("hqa", s - 1, ha[:].rearrange("p c n -> p (c n)"), 2 * P)
-            hy = copy_turned("hy", bank_b, 0, 2 if live(s - 4) else 1)
             if live(s - 3):
-                round_y(s - 3)
-            if live(s + 2):
-                sort_x(s + 2)
-            if rt == 1:
-                copy_fac(g, bank_s)
+                square(s - 3)
+                finish_y(s - 3, nc.gpsimd)
+                round_y(s - 3, pool_cast)
+            ha = copy_turned("ha", bank_a, 0, 2)
+            hy = copy_turned("hy", bank_b, 0, 2 if live(s - 4) else 1)
+            if live(s + 3):
+                sort_x(s + 3)
             for j in range(FP):
                 weight_h(s, j)
+            quantize("hqa", s - 1, ha[:].rearrange("p c n -> p (c n)"), 2 * P)
             quantize("hqb", s - 1, hy[:, 0, :], P)
             if live(s - 4):
                 quantize_y(s - 4, hy[:, 1, :])
                 if rt == RT - 1:
                     store_codes(g - 1, 0, R)
                     store_scales(g - 1, [nc.sync] * 4)
-            if rt == 2 and g + 1 < G:
-                copy_isq(g + 1, 0, 2, bank_s)
-            if rt == 3 and g + 1 < G:
-                copy_isq(g + 1, 2, 3, bank_s)
+            if s == max(RT * g + 1, 2):
+                nc.vector.scalar_tensor_tensor(out=fac[g][:], in0=oc[g][:], scalar=1.0, in1=vf[g][:], op0=ALU.add, op1=ALU.mult)
             if live(s - 2):
                 stage2(s - 2)
 
@@ -357,7 +349,7 @@ def tile_grouped_raman_intensities_k7_kernel(
         t["yb", last] = yb
         round_y(last - 1)
         turned = []
-        for n, name in enumerate(["ps_ta", "ps_tb", "ps_x"]):
+        for n, name in enumerate(["ps_ta", "ps_tb", "ps_h2"]):
             bank = psum.tile([P, 2, 2, P], F32, name=name)
             transpose_pair(bank, 0, t["yb", last - 2 + n])
             turned.append(bank)

@@ -17,12 +17,26 @@ ALU = mybir.AluOpType
 ACT = mybir.ActivationFunctionType
 
 P = 128
-PASS = 512
-KP = K // PASS
-FP = F // PASS
-RT = R // P
-TILES = G * RT
-UNSORTED = 2
+CHUNK = 512
+K_CHUNKS = K // CHUNK
+F_CHUNKS = F // CHUNK
+TILES_PER_MOL = R // P
+TILES = G * TILES_PER_MOL
+LAST = TILES - 1
+QUADRANT = 32
+UNSORTED_TILES = 2
+LOAD_AHEAD = 6
+SORT_AHEAD = 4
+TURN_AHEAD = 2
+STAGE2_BEHIND = 2
+EPILOGUE_BEHIND = 3
+PLANES_BEHIND = 4
+
+J_SCALE_RUNS = {0: 1, 1: 2, 2: G}
+L_SCALE_RUNS = {0: 1, 1: G}
+
+NATURAL = "r (p u e) -> r u p e"
+SORTED = "r (u p e) -> r u p e"
 
 
 def tile_grouped_raman_intensities_k7_kernel(
@@ -35,80 +49,128 @@ def tile_grouped_raman_intensities_k7_kernel(
         psum = ctx.enter_context(tc.psum_pool(name="psum", bufs=1))
         ctx.enter_context(tc.manual_schedule())
 
+        def scale_tiles(name, runs, chunks, width):
+            return {
+                lo: keep.tile([P, (hi - lo) * chunks, width], U8, name="%s%d" % (name, lo), align_bytes=64)
+                for lo, hi in runs.items()
+            }
+
+        def scale_plane(tiles, chunks, g, c):
+            lo = max(first for first in tiles if first <= g)
+            return tiles[lo][:, (g - lo) * chunks + c, :]
+
         x_raw = [keep.tile([P, K], BF16, name="x_raw%d" % i, align_bytes=64) for i in range(TILES)]
-        j_words = [[keep.tile([P, KP, 2 * PASS], U8, name="j_words%d_%d" % (g, j), align_bytes=64) for j in range(FP)] for g in range(G)]
-        j_scales = [keep.tile([P, KP, F], U8, name="j_scales%d" % g, align_bytes=64) for g in range(G)]
-        l_words = [keep.tile([P, FP, 2 * M], U8, name="l_words%d" % g, align_bytes=64) for g in range(G)]
-        l_scales = [keep.tile([P, FP, M], U8, name="l_scales%d" % g, align_bytes=64) for g in range(G)]
+        j_first = [keep.tile([P, K_CHUNKS, 2 * CHUNK], U8, name="j_first%d" % j, align_bytes=64) for j in range(F_CHUNKS)]
+        j_later = {g: keep.tile([P, K_CHUNKS, 2 * F], U8, name="j_words%d" % g, align_bytes=64) for g in range(1, G)}
+        j_scales = scale_tiles("j_scales", J_SCALE_RUNS, K_CHUNKS, F)
+        l_words = [keep.tile([P, F_CHUNKS, 2 * M], U8, name="l_words%d" % g, align_bytes=64) for g in range(G)]
+        l_scales = scale_tiles("l_scales", L_SCALE_RUNS, F_CHUNKS, M)
         isq = [keep.tile([P, F], BF16, name="isq%d" % g, align_bytes=64) for g in range(G)]
-        isq_col = keep.tile([P, FP, 4], BF16, name="isq_col", align_bytes=64)
+        isq_col = keep.tile([P, F_CHUNKS, 4], BF16, name="isq_col", align_bytes=64)
         vf = [keep.tile([P, M], BF16, name="vf%d" % g, align_bytes=64) for g in range(G)]
         oc = [keep.tile([P, M], BF16, name="oc%d" % g, align_bytes=64) for g in range(G)]
         fac = [keep.tile([P, M], F32, name="fac%d" % g, align_bytes=64) for g in range(G)]
         y_codes = [keep.tile([P, R], U32, name="y_codes%d" % g, align_bytes=64) for g in range(G)]
         y_scales = [keep.tile([P, R], U8, name="y_scales%d" % g, align_bytes=64) for g in range(G)]
-        ident0 = keep.tile([P, P], F32, name="ident0", align_bytes=64)
+        ident_raw = keep.tile([P, P], F32, name="ident_raw", align_bytes=64)
         ident = keep.tile([P, P], F32, name="ident", align_bytes=64)
 
         out_words = out_1[0].rearrange("p m t -> p (m t)")
 
-        def load_x(i):
-            g, rt = divmod(i, RT)
-            nc.sync.dma_start(out=x_raw[i][:], in_=dalpha[g, rt * P:(rt + 1) * P, :])
+        x_sorted, x_bank, x_turned, x_quant = {}, {}, {}, {}
+        h_bank, h_bf16, h_quant_01, h_quant_2 = {}, {}, {}, {}
+        d_bank, d_squared, y_f32, y_bf16 = {}, {}, {}, {}
 
-        def load_scales(tile, src, passes, g):
+        def live(i):
+            return 0 <= i < TILES
+
+
+        def load_x(i):
+            g, n = divmod(i, TILES_PER_MOL)
+            nc.sync.dma_start(out=x_raw[i][:], in_=dalpha[g, n * P:(n + 1) * P, :])
+
+        def load_scales(tiles, src, runs, chunks, g):
             for r in range(4):
                 nc.sync.dma_start(
-                    out=tile[r:P:32, :, :].bitcast(I32),
-                    in_=src[passes * g:passes * (g + 1), r:16:4, :].rearrange("g q n -> q g n").bitcast(I32),
+                    out=tiles[g][r:P:QUADRANT, :, :].bitcast(I32),
+                    in_=src[chunks * g:chunks * runs[g], r:16:4, :].rearrange("g q n -> q g n").bitcast(I32),
                 )
 
-        def load_j(g, j):
+        def load_j(tile, g, cols):
             nc.sync.dma_start(
-                out=j_words[g][j][:].bitcast(I32),
-                in_=jac_words[KP * g:KP * (g + 1), :, 2 * PASS * j:2 * PASS * (j + 1)].rearrange("g p n -> p g n").bitcast(I32),
+                out=tile[:].bitcast(I32),
+                in_=jac_words[K_CHUNKS * g:K_CHUNKS * (g + 1), :, cols].rearrange("g p n -> p g n").bitcast(I32),
             )
 
         def load_l(g):
             nc.sync.dma_start(
                 out=l_words[g][:].bitcast(I32),
-                in_=mode_words[FP * g:FP * (g + 1), :, :].rearrange("g p n -> p g n").bitcast(I32),
+                in_=mode_words[F_CHUNKS * g:F_CHUNKS * (g + 1), :, :].rearrange("g p n -> p g n").bitcast(I32),
             )
 
         def load_row(tile, src, g):
             nc.sync.dma_start(out=tile[:], in_=src[g].partition_broadcast(P))
 
-        def first_stage_loads(g):
-            load_scales(j_scales[g], jac_scales, KP, g)
-            for j in range(FP):
-                load_j(g, j)
-            if g > 0:
-                load_row(isq[g], isqm, g)
+        def load_stage1_operands(g):
+            if g in J_SCALE_RUNS:
+                load_scales(j_scales, jac_scales, J_SCALE_RUNS, K_CHUNKS, g)
+            load_j(j_later[g], g, slice(0, 2 * F))
+            load_row(isq[g], isqm, g)
 
-        def second_stage_loads(g):
-            load_scales(l_scales[g], mode_scales, FP, g)
+        def load_stage2_operands(g):
+            if g in L_SCALE_RUNS:
+                load_scales(l_scales, mode_scales, L_SCALE_RUNS, F_CHUNKS, g)
             load_l(g)
             load_row(oc[g], occ, g)
             load_row(vf[g], vfac, g)
 
-        t = {}
+
+        def new_bank(name):
+            return psum.tile([P, 2, 2, P], F32, name=name, bufs=2 if name == "ps_d" else 1)
+
+        def turn(bank, half, sorted_chunk):
+            words = sorted_chunk[:].bitcast(F32)
+            for u in range(2):
+                nc.tensor.transpose(bank[:, half, u, :], words[:, u * P:(u + 1) * P], ident[:])
+
+        def copy_out(dst, src, move=nc.scalar.copy):
+            move(out=dst.bitcast(F32).rearrange("p c (r u) -> p c r u", u=2), in_=src.rearrange("p c u r -> p c r u"))
+
+        def copy_halves(name, bank, lo, hi, move=nc.scalar.copy):
+            dst = work.tile([P, 2, CHUNK], BF16, name=name, align_bytes=64)
+            copy_out(dst[:, lo:hi, :], bank[:, lo:hi, :, :], move)
+            return dst
+
+        def quantize(name, src, chunks):
+            codes = work.tile([P, chunks * P], U32, name=name + "_codes", align_bytes=64)
+            scales = work.tile([P, chunks * P], U8, name=name + "_scales", align_bytes=64)
+            nc.vector.quantize_mx(out=codes[:].bitcast(FP8X4), scales=scales[:], in_=src)
+            return codes, scales
+
 
         def sort_x(i):
-            xs = work.tile([P, KP, 2, P], F32, name="xs", align_bytes=64)
-            nc.scalar.copy(out=xs[:], in_=x_raw[i][:].bitcast(F32).rearrange("r (c p u) -> r c u p", c=KP, u=2))
-            t["xs", i] = xs
+            xs = work.tile([P, K_CHUNKS, 2, P], F32, name="xs", align_bytes=64)
+            nc.scalar.copy(out=xs[:], in_=x_raw[i][:].bitcast(F32).rearrange("r (c p u) -> r c u p", p=P, u=2))
+            x_sorted[i] = xs
 
-        def transpose_x(i):
-            bank = psum.tile([P, KP, 2, P], F32, name="ps_x", bufs=2)
-            words = x_raw[i][:].bitcast(F32)
-            for c in range(KP):
+        def turn_x(i, name="ps_x"):
+            bank = new_bank(name)
+            words = x_raw[i][:].bitcast(F32).rearrange("r (c p u) -> r c u p", p=P, u=2)
+            for c in range(K_CHUNKS):
                 for u in range(2):
-                    src = t["xs", i][:, c, u, :] if i >= UNSORTED else words[:, 256 * c + u:256 * (c + 1):2]
+                    src = words[:, c, u, :] if i < UNSORTED_TILES else x_sorted[i][:, c, u, :]
                     nc.tensor.transpose(bank[:, c, u, :], src, ident[:])
-            t["ps_x", i] = bank
+            x_bank[i] = bank
+
+        def copy_x(i):
+            x_turned[i] = copy_halves("xg", x_bank[i], 0, K_CHUNKS)
+
+        def quantize_x(i):
+            x_quant[i] = quantize("xq", x_turned[i][:].rearrange("p c n -> p (c n)"), K_CHUNKS)
+
 
         def spread_isq(lo, hi, name):
-            bank = psum.tile([P, 2, 2, P], F32, name=name)
+            bank = new_bank(name)
             for j in range(lo, hi):
                 words = isq_col[:, j, :].bitcast(F32)
                 for u in range(2):
@@ -117,111 +179,84 @@ def tile_grouped_raman_intensities_k7_kernel(
 
         def copy_isq(lo, hi, bank):
             nc.vector.tensor_copy(
-                out=isq[0][:, lo * PASS:hi * PASS].bitcast(F32).rearrange("r (j p u) -> r j p u", p=P, u=2),
+                out=isq[0][:, lo * CHUNK:hi * CHUNK].bitcast(F32).rearrange("r (j p u) -> r j p u", p=P, u=2),
                 in_=bank[:, 0:hi - lo, :, :].rearrange("r j u p -> r j p u"),
             )
 
-        def copy_x(i):
-            xg = work.tile([P, KP * PASS], BF16, name="xg", align_bytes=64)
-            nc.scalar.copy(
-                out=xg[:].bitcast(F32).rearrange("p (c r u) -> p c r u", c=KP, u=2),
-                in_=t["ps_x", i][:].rearrange("p c u r -> p c r u"),
-            )
-            t["xg", i] = xg
-
-        def quantize(name, i, src, width):
-            codes = work.tile([P, width], U32, name=name + "_codes", align_bytes=64)
-            scales = work.tile([P, width], U8, name=name + "_scales", align_bytes=64)
-            nc.vector.quantize_mx(out=codes[:].bitcast(FP8X4), scales=scales[:], in_=src)
-            t[name, i] = (codes, scales)
 
         def stage1(i):
-            g = i // RT
-            codes, scales = t["xq", i]
-            for j in range(FP):
-                bank = psum.tile([P, PASS], F32, name="ps_h%d" % j)
-                for c in range(KP):
+            g = i // TILES_PER_MOL
+            codes, scales = x_quant[i]
+            for j in range(F_CHUNKS):
+                bank = psum.tile([P, CHUNK], F32, name="ps_h%d" % j)
+                for c in range(K_CHUNKS):
+                    words = j_first[j][:, c, :] if g == 0 else j_later[g][:, c, 2 * CHUNK * j:2 * CHUNK * (j + 1)]
                     nc.tensor.matmul_mx(
                         out=bank[:],
                         lhsT=codes[:, c * P:(c + 1) * P].bitcast(FP8X4),
                         lhsT_scale=scales[:, c * P:(c + 1) * P],
-                        rhs=j_words[g][j][:, c, :].bitcast(FP4X4),
-                        rhs_scale=j_scales[g][:, c, j * PASS:(j + 1) * PASS],
+                        rhs=words.bitcast(FP4X4),
+                        rhs_scale=scale_plane(j_scales, K_CHUNKS, g, c)[:, j * CHUNK:(j + 1) * CHUNK],
                         start=(c == 0),
-                        stop=(c == KP - 1),
+                        stop=(c == K_CHUNKS - 1),
                     )
-                t["ps_h", i, j] = bank
+                h_bank[i, j] = bank
 
-        def weight_h(i, j):
-            g = i // RT
-            hb = work.tile([P, PASS], BF16, name="hb%d" % j, align_bytes=64)
-            nc.vector.tensor_tensor(
-                out=hb[:].rearrange("r (u p e) -> r u p e", u=2, e=2),
-                in0=t["ps_h", i, j][:].rearrange("r (p u e) -> r u p e", u=2, e=2),
-                in1=isq[g][:, j * PASS:(j + 1) * PASS].rearrange("r (p u e) -> r u p e", u=2, e=2),
-                op=ALU.mult,
-            )
-            t["hb", i, j] = hb
-
-        def transpose_pair(bank, half, src):
-            words = src[:].bitcast(F32)
-            for u in range(2):
-                nc.tensor.transpose(bank[:, half, u, :], words[:, u * P:(u + 1) * P], ident[:])
-
-        def copy_turned(name, bank, lo, hi, move=nc.scalar.copy):
-            dst = work.tile([P, 2, PASS], BF16, name=name, align_bytes=64)
-            move(
-                out=dst[:, lo:hi, :].bitcast(F32).rearrange("p c (r u) -> p c r u", u=2),
-                in_=bank[:, lo:hi, :, :].rearrange("p c u r -> p c r u"),
-            )
-            return dst
+        def weight_h(i):
+            for j in range(F_CHUNKS):
+                hb = work.tile([P, CHUNK], BF16, name="hb%d" % j, align_bytes=64)
+                nc.vector.tensor_tensor(
+                    out=hb[:].rearrange(SORTED, u=2, e=2),
+                    in0=h_bank[i, j][:].rearrange(NATURAL, u=2, e=2),
+                    in1=isq[i // TILES_PER_MOL][:, j * CHUNK:(j + 1) * CHUNK].rearrange(NATURAL, u=2, e=2),
+                    op=ALU.mult,
+                )
+                h_bf16[i, j] = hb
 
         def stage2(i, name="ps_d"):
-            g = i // RT
-            bank = psum.tile([P, M], F32, name=name)
-            for j in range(FP):
-                codes, scales = t["hqa", i] if j < 2 else t["hqb", i]
-                c = j % 2
+            g = i // TILES_PER_MOL
+            bank = new_bank(name)[:].rearrange("r a b c -> r (a b c)")
+            order = [0, 1, 2] if i == LAST else [2, 1, 0]
+            for j in order:
+                codes, scales = h_quant_01[i] if j < 2 else h_quant_2[i]
+                cols = slice((j % 2) * P, (j % 2 + 1) * P)
                 nc.tensor.matmul_mx(
-                    out=bank[:],
-                    lhsT=codes[:, c * P:(c + 1) * P].bitcast(FP8X4),
-                    lhsT_scale=scales[:, c * P:(c + 1) * P],
+                    out=bank,
+                    lhsT=codes[:, cols].bitcast(FP8X4),
+                    lhsT_scale=scales[:, cols],
                     rhs=l_words[g][:, j, :].bitcast(FP4X4),
-                    rhs_scale=l_scales[g][:, j, :],
-                    start=(j == 0),
-                    stop=(j == FP - 1),
+                    rhs_scale=scale_plane(l_scales, F_CHUNKS, g, j),
+                    start=(j == order[0]),
+                    stop=(j == order[-1]),
                 )
-            t["ps_d", i] = bank
+            d_bank[i] = bank
+
+        def make_factor(g, cols):
+            nc.vector.scalar_tensor_tensor(
+                out=fac[g][:, cols], in0=oc[g][:, cols], scalar=1.0, in1=vf[g][:, cols], op0=ALU.add, op1=ALU.mult
+            )
 
         def square(i):
             sq = work.tile([P, M], F32, name="sq", align_bytes=64)
-            nc.scalar.activation(out=sq[:], in_=t["ps_d", i][:], func=ACT.Square)
-            t["sq", i] = sq
+            nc.scalar.activation(out=sq[:], in_=d_bank[i], func=ACT.Square)
+            d_squared[i] = sq
 
-        def finish_y(i, engine=nc.vector):
-            g, rt = divmod(i, RT)
-            y = work.tile([P, M], F32, name="y", align_bytes=64, bufs=4)
-            engine.tensor_tensor(out=y[:], in0=t["sq", i][:], in1=fac[g][:], op=ALU.mult)
-            nc.sync.dma_start(out=out_0[g, rt * P:(rt + 1) * P, :], in_=y[:])
-            t["y", i] = y
+        def finish_y(i):
+            g, n = divmod(i, TILES_PER_MOL)
+            y = work.tile([P, M], F32, name="y", align_bytes=64, bufs=6)
+            nc.vector.tensor_tensor(out=y[:], in0=d_squared[i][:], in1=fac[g][:], op=ALU.mult)
+            nc.sync.dma_start(out=out_0[g, n * P:(n + 1) * P, :], in_=y[:])
+            y_f32[i] = y
 
         def round_y(i, move=nc.scalar.copy):
             yb = work.tile([P, M], BF16, name="yb", align_bytes=64)
-            move(
-                out=yb[:].rearrange("r (u p e) -> r u p e", u=2, e=2),
-                in_=t["y", i][:].rearrange("r (p u e) -> r u p e", u=2, e=2),
-            )
-            t["yb", i] = yb
-
-        def pool_cast(out, in_):
-            nc.gpsimd.tensor_scalar(out=out, in0=in_, scalar1=1.0, scalar2=0.0, op0=ALU.mult, op1=ALU.add)
+            move(out=yb[:].rearrange(SORTED, u=2, e=2), in_=y_f32[i][:].rearrange(NATURAL, u=2, e=2))
+            y_bf16[i] = yb
 
         def quantize_y(i, src):
-            g, rt = divmod(i, RT)
+            g, n = divmod(i, TILES_PER_MOL)
             nc.vector.quantize_mx(
-                out=y_codes[g][:, rt * P:(rt + 1) * P].bitcast(FP8X4),
-                scales=y_scales[g][:, rt * P:(rt + 1) * P],
-                in_=src,
+                out=y_codes[g][:, n * P:(n + 1) * P].bitcast(FP8X4), scales=y_scales[g][:, n * P:(n + 1) * P], in_=src
             )
 
         def store_codes(g, lo, hi):
@@ -233,133 +268,156 @@ def tile_grouped_raman_intensities_k7_kernel(
             for q in range(4):
                 queues[q].dma_start(
                     out=out_2[0, 4 * q:4 * q + 4, R * g:R * (g + 1)].bitcast(I32),
-                    in_=y_scales[g][32 * q:32 * q + 4, :].bitcast(I32),
+                    in_=y_scales[g][QUADRANT * q:QUADRANT * q + 4, :].bitcast(I32),
                 )
 
-        def live(i):
-            return 0 <= i < TILES
 
-        make_identity(nc, ident0[:])
-        nc.scalar.activation(out=ident[:], in_=ident0[:], func=ACT.Square)
-        for g in range(G):
-            nc.vector.memset(j_scales[g][:].bitcast(I32), 0)
-            nc.vector.memset(l_scales[g][:].bitcast(I32), 0)
+        make_identity(nc, ident_raw[:])
+        nc.scalar.activation(out=ident[:], in_=ident_raw[:], func=ACT.Square)
+        for tile in (j_scales[0], l_scales[0], j_scales[1], l_scales[1], j_scales[2]):
+            nc.vector.memset(tile[:].bitcast(I32), 0)
         load_x(0)
         nc.sync.dma_start(out=isq_col[:], in_=isqm[0].rearrange("(j p t) -> p j t", p=P, t=4))
         load_x(1)
-        first_stage_loads(0)
-        load_x(2)
-        load_x(3)
-        load_x(4)
-        second_stage_loads(0)
-        load_x(5)
+        load_scales(j_scales, jac_scales, J_SCALE_RUNS, K_CHUNKS, 0)
+        for j in range(F_CHUNKS):
+            load_j(j_first[j], 0, slice(2 * CHUNK * j, 2 * CHUNK * (j + 1)))
+        for i in range(2, LOAD_AHEAD):
+            load_x(i)
+        load_scales(l_scales, mode_scales, L_SCALE_RUNS, F_CHUNKS, 0)
+        load_l(0)
+        load_x(LOAD_AHEAD)
+        load_row(oc[0], occ, 0)
+        load_row(vf[0], vfac, 0)
 
-        transpose_x(0)
-        first_a = spread_isq(0, 2, "ps_ta")
-        first_b = spread_isq(2, 3, "ps_tb")
+        turn_x(0)
+        isq_bank_01 = spread_isq(0, 2, "ps_ta")
+        isq_bank_2 = spread_isq(2, 3, "ps_tb")
         copy_x(0)
-        quantize("xq", 0, t["xg", 0][:], KP * P)
-        transpose_x(1)
-        copy_isq(0, 2, first_a)
-        copy_isq(2, 3, first_b)
+        quantize_x(0)
+        turn_x(1, "ps_d")
+        copy_isq(0, 2, isq_bank_01)
+        copy_isq(2, 3, isq_bank_2)
         copy_x(1)
         stage1(0)
-        quantize("xq", 1, t["xg", 1][:], KP * P)
-        sort_x(2)
-        sort_x(3)
-        for j in range(FP):
-            weight_h(0, j)
+        quantize_x(1)
+        for i in range(UNSORTED_TILES, SORT_AHEAD):
+            sort_x(i)
+        turn_x(2, "ps_d")
+        copy_x(2)
+        sort_x(SORT_AHEAD)
+        weight_h(0)
+        quantize_x(2)
+
 
         for s in range(1, TILES):
-            g, rt = divmod(s, RT)
-            if live(s + 5):
-                load_x(s + 5)
-            if g + 1 < G and rt == 1:
-                first_stage_loads(g + 1)
-            if g + 1 < G and rt == 3:
-                second_stage_loads(g + 1)
+            g, n = divmod(s, TILES_PER_MOL)
+            x_tile, h_tile, e_tile, y_tile = s + TURN_AHEAD, s - 1, s - EPILOGUE_BEHIND, s - PLANES_BEHIND
+            if live(s + LOAD_AHEAD):
+                load_x(s + LOAD_AHEAD)
+            if g + 1 < G and n == 1:
+                load_stage1_operands(g + 1)
+            if g + 1 < G and n == 3:
+                load_stage2_operands(g + 1)
 
-            if live(s + 1):
-                transpose_x(s + 1)
-            bank_a = psum.tile([P, 2, 2, P], F32, name="ps_ta")
-            transpose_pair(bank_a, 0, t["hb", s - 1, 0])
-            transpose_pair(bank_a, 1, t["hb", s - 1, 1])
-            bank_b = psum.tile([P, 2, 2, P], F32, name="ps_tb")
-            transpose_pair(bank_b, 0, t["hb", s - 1, 2])
-            if live(s - 4):
-                transpose_pair(bank_b, 1, t["yb", s - 4])
-
-            if live(s + 1):
-                copy_x(s + 1)
-                quantize("xq", s + 1, t["xg", s + 1][:], KP * P)
+            bank_b = new_bank("ps_tb")
+            if live(y_tile):
+                turn(bank_b, 1, y_bf16[y_tile])
+            if live(x_tile):
+                turn_x(x_tile)
+            chunk2_first = live(h_tile - STAGE2_BEHIND) and live(x_tile)
+            if chunk2_first:
+                turn(bank_b, 0, h_bf16[h_tile, 2])
+            bank_a = new_bank("ps_ta")
+            turn(bank_a, 0, h_bf16[h_tile, 0])
+            turn(bank_a, 1, h_bf16[h_tile, 1])
+            if not chunk2_first:
+                turn(bank_b, 0, h_bf16[h_tile, 2])
             stage1(s)
-            if live(s - 3):
-                square(s - 3)
-                finish_y(s - 3, nc.gpsimd)
-                round_y(s - 3, pool_cast)
-            ha = copy_turned("ha", bank_a, 0, 2)
-            hy = copy_turned("hy", bank_b, 0, 2 if live(s - 4) else 1)
-            if live(s + 3):
-                sort_x(s + 3)
-            for j in range(FP):
-                weight_h(s, j)
-            quantize("hqa", s - 1, ha[:].rearrange("p c n -> p (c n)"), 2 * P)
-            quantize("hqb", s - 1, hy[:, 0, :], P)
-            if live(s - 4):
-                quantize_y(s - 4, hy[:, 1, :])
-                if rt == RT - 1:
-                    store_codes(g - 1, 0, R)
-                    store_scales(g - 1, [nc.sync] * 4)
-            if s == max(RT * g + 1, 2):
-                nc.vector.scalar_tensor_tensor(out=fac[g][:], in0=oc[g][:], scalar=1.0, in1=vf[g][:], op0=ALU.add, op1=ALU.mult)
-            if live(s - 2):
-                stage2(s - 2)
 
-        last = TILES - 1
-        bank_a = psum.tile([P, 2, 2, P], F32, name="ps_ta")
-        transpose_pair(bank_a, 0, t["hb", last, 0])
-        transpose_pair(bank_a, 1, t["hb", last, 1])
-        bank_b = psum.tile([P, 2, 2, P], F32, name="ps_tb")
-        transpose_pair(bank_b, 0, t["hb", last, 2])
-        transpose_pair(bank_b, 1, t["yb", last - 3])
-        square(last - 2)
-        ha = copy_turned("ha", bank_a, 0, 2)
-        hy = copy_turned("hy", bank_b, 0, 2)
-        finish_y(last - 2)
-        quantize("hqa", last, ha[:].rearrange("p c n -> p (c n)"), 2 * P)
-        round_y(last - 2, nc.vector.tensor_copy)
-        stage2(last - 1, "ps_h0")
-        square(last - 1)
-        quantize("hqb", last, hy[:, 0, :], P)
-        quantize_y(last - 3, hy[:, 1, :])
-        stage2(last, "ps_h1")
-        finish_y(last - 1)
+            hx = work.tile([P, 2 + K_CHUNKS, CHUNK], BF16, name="hx", align_bytes=64)
+            if live(e_tile):
+                square(e_tile)
+                finish_y(e_tile)
+            if live(x_tile):
+                copy_out(hx[:, 2:2 + K_CHUNKS, :], x_bank[x_tile][:])
+            copy_out(hx[:, 0:2, :], bank_a[:])
+            hy = copy_halves("hy", bank_b, 0, 2 if live(y_tile) else 1)
+            if live(e_tile):
+                round_y(e_tile)
+            if live(s + SORT_AHEAD):
+                sort_x(s + SORT_AHEAD)
+            weight_h(s)
+            chunks = 2 + K_CHUNKS if live(x_tile) else 2
+            hx_codes = work.tile([P, (2 + K_CHUNKS) * P], U32, name="hx_codes", align_bytes=64, bufs=4)
+            hx_scales = work.tile([P, (2 + K_CHUNKS) * P], U8, name="hx_scales", align_bytes=64, bufs=4)
+            nc.vector.quantize_mx(
+                out=hx_codes[:, 0:chunks * P].bitcast(FP8X4),
+                scales=hx_scales[:, 0:chunks * P],
+                in_=hx[:, 0:chunks, :].rearrange("p c n -> p (c n)"),
+            )
+            h_quant_01[h_tile] = (hx_codes[:, 0:2 * P], hx_scales[:, 0:2 * P])
+            x_quant[x_tile] = (hx_codes[:, 2 * P:], hx_scales[:, 2 * P:])
+            h_quant_2[h_tile] = quantize("h2", hy[:, 0, :], 1)
+            if live(y_tile):
+                quantize_y(y_tile, hy[:, 1, :])
+                if y_tile % TILES_PER_MOL == TILES_PER_MOL - 1:
+                    store_codes(y_tile // TILES_PER_MOL, 0, R)
+                    store_scales(y_tile // TILES_PER_MOL, [nc.sync] * 4)
+            if g == 0 and n == 2:
+                make_factor(g, slice(0, M))
+            if g > 0 and n in (1, 2):
+                make_factor(g, slice((n - 1) * M // 2, n * M // 2))
+            if live(s - STAGE2_BEHIND):
+                stage2(s - STAGE2_BEHIND)
+
+
+        bank_a = new_bank("ps_ta")
+        turn(bank_a, 0, h_bf16[LAST, 0])
+        turn(bank_a, 1, h_bf16[LAST, 1])
+        bank_b = new_bank("ps_tb")
+        turn(bank_b, 0, h_bf16[LAST, 2])
+        turn(bank_b, 1, y_bf16[LAST - 3])
+        square(LAST - 2)
+        h01 = copy_halves("ha", bank_a, 0, 2)
+        hy = copy_halves("hy", bank_b, 0, 2)
+        finish_y(LAST - 2)
+        h_quant_01[LAST] = quantize("h01", h01[:].rearrange("p c n -> p (c n)"), 2)
+        round_y(LAST - 2, nc.vector.tensor_copy)
+        stage2(LAST - 1, "ps_h0")
+        square(LAST - 1)
+        h_quant_2[LAST] = quantize("h2", hy[:, 0, :], 1)
+        quantize_y(LAST - 3, hy[:, 1, :])
+        stage2(LAST, "ps_h1")
+        finish_y(LAST - 1)
+
         sq = work.tile([P, M], F32, name="sq", align_bytes=64)
         yb = work.tile([P, M], BF16, name="yb", align_bytes=64)
         for h in range(2):
             cols = slice(h * M // 2, (h + 1) * M // 2)
-            nc.scalar.activation(out=sq[:, cols], in_=t["ps_d", last][:, cols], func=ACT.Square)
+            nc.scalar.activation(out=sq[:, cols], in_=d_bank[LAST][:, cols], func=ACT.Square)
             nc.vector.tensor_tensor(
-                out=yb[:].rearrange("r (u p e) -> r u p e", u=2, e=2)[:, :, h * P // 2:(h + 1) * P // 2, :],
-                in0=sq[:, cols].rearrange("r (p u e) -> r u p e", u=2, e=2),
-                in1=fac[G - 1][:, cols].rearrange("r (p u e) -> r u p e", u=2, e=2),
+                out=yb[:].rearrange(SORTED, u=2, e=2)[:, :, h * P // 2:(h + 1) * P // 2, :],
+                in0=sq[:, cols].rearrange(NATURAL, u=2, e=2),
+                in1=fac[G - 1][:, cols].rearrange(NATURAL, u=2, e=2),
                 op=ALU.mult,
             )
-        t["sq", last] = sq
-        t["yb", last] = yb
-        round_y(last - 1)
-        turned = []
-        for n, name in enumerate(["ps_ta", "ps_tb", "ps_h2"]):
-            bank = psum.tile([P, 2, 2, P], F32, name=name)
-            transpose_pair(bank, 0, t["yb", last - 2 + n])
-            turned.append(bank)
-        y_a = copy_turned("ha", turned[0], 0, 1)
-        y_b = copy_turned("hy", turned[1], 0, 1)
-        finish_y(last)
-        quantize_y(last - 2, y_a[:, 0, :])
-        y_c = copy_turned("ha", turned[2], 0, 1, nc.vector.tensor_copy)
-        quantize_y(last - 1, y_b[:, 0, :])
+        d_squared[LAST] = sq
+        y_bf16[LAST] = yb
+        round_y(LAST - 1)
+
+        y_banks = []
+        for i, name in zip(range(LAST - 2, TILES), ["ps_ta", "ps_tb", "ps_h2"]):
+            bank = new_bank(name)
+            turn(bank, 0, y_bf16[i])
+            y_banks.append(bank)
+        y_turned_0 = copy_halves("ha", y_banks[0], 0, 1)
+        y_turned_1 = copy_halves("hy", y_banks[1], 0, 1)
+        finish_y(LAST)
+        quantize_y(LAST - 2, y_turned_0[:, 0, :])
+        y_turned_2 = copy_halves("ha", y_banks[2], 0, 1, nc.vector.tensor_copy)
+        quantize_y(LAST - 1, y_turned_1[:, 0, :])
         store_codes(G - 1, 0, R - P)
-        quantize_y(last, y_c[:, 0, :])
+        quantize_y(LAST, y_turned_2[:, 0, :])
         store_codes(G - 1, R - P, R)
         store_scales(G - 1, [nc.scalar, nc.scalar, nc.sync, nc.sync])

from contextlib import ExitStack

import concourse.mybir as mybir
from concourse.masks import make_identity

G, R, K, F, M = 4, 512, 1024, 1536, 512
FLOPS = 2 * G * R * (K * F + F * M)

F32 = mybir.dt.float32
BF16 = mybir.dt.bfloat16
I32 = mybir.dt.int32
U32 = mybir.dt.uint32
U8 = mybir.dt.uint8
FP8X4 = mybir.dt.float8_e4m3fn_x4
FP4X4 = mybir.dt.float4_e2m1fn_x4
ALU = mybir.AluOpType
ACT = mybir.ActivationFunctionType

P = 128
CHUNK = 512
K_CHUNKS = K // CHUNK
F_CHUNKS = F // CHUNK
TILES_PER_MOL = R // P
TILES = G * TILES_PER_MOL
LAST = TILES - 1
QUADRANT = 32
UNSORTED_TILES = 2
LOAD_AHEAD = 6
SORT_AHEAD = 4
TURN_AHEAD = 2
STAGE2_BEHIND = 2
EPILOGUE_BEHIND = 3
PLANES_BEHIND = 4

J_SCALE_RUNS = {0: 1, 1: 2, 2: G}
L_SCALE_RUNS = {0: 1, 1: G}

NATURAL = "r (p u e) -> r u p e"
SORTED = "r (u p e) -> r u p e"


def tile_grouped_raman_intensities_k7_kernel(
    tc, dalpha, jac_words, jac_scales, isqm, mode_words, mode_scales, vfac, occ, out_0, out_1, out_2
):
    nc = tc.nc
    with ExitStack() as ctx:
        keep = ctx.enter_context(tc.tile_pool(name="keep", bufs=1))
        work = ctx.enter_context(tc.tile_pool(name="work", bufs=3))
        psum = ctx.enter_context(tc.psum_pool(name="psum", bufs=1))
        ctx.enter_context(tc.manual_schedule())

        def scale_tiles(name, runs, chunks, width):
            return {
                lo: keep.tile([P, (hi - lo) * chunks, width], U8, name="%s%d" % (name, lo), align_bytes=64)
                for lo, hi in runs.items()
            }

        def scale_plane(tiles, chunks, g, c):
            lo = max(first for first in tiles if first <= g)
            return tiles[lo][:, (g - lo) * chunks + c, :]

        x_raw = [keep.tile([P, K], BF16, name="x_raw%d" % i, align_bytes=64) for i in range(TILES)]
        j_first = [keep.tile([P, K_CHUNKS, 2 * CHUNK], U8, name="j_first%d" % j, align_bytes=64) for j in range(F_CHUNKS)]
        j_later = {g: keep.tile([P, K_CHUNKS, 2 * F], U8, name="j_words%d" % g, align_bytes=64) for g in range(1, G)}
        j_scales = scale_tiles("j_scales", J_SCALE_RUNS, K_CHUNKS, F)
        l_words = [keep.tile([P, F_CHUNKS, 2 * M], U8, name="l_words%d" % g, align_bytes=64) for g in range(G)]
        l_scales = scale_tiles("l_scales", L_SCALE_RUNS, F_CHUNKS, M)
        isq = [keep.tile([P, F], BF16, name="isq%d" % g, align_bytes=64) for g in range(G)]
        isq_col = keep.tile([P, F_CHUNKS, 4], BF16, name="isq_col", align_bytes=64)
        vf = [keep.tile([P, M], BF16, name="vf%d" % g, align_bytes=64) for g in range(G)]
        oc = [keep.tile([P, M], BF16, name="oc%d" % g, align_bytes=64) for g in range(G)]
        fac = [keep.tile([P, M], F32, name="fac%d" % g, align_bytes=64) for g in range(G)]
        y_codes = [keep.tile([P, R], U32, name="y_codes%d" % g, align_bytes=64) for g in range(G)]
        y_scales = [keep.tile([P, R], U8, name="y_scales%d" % g, align_bytes=64) for g in range(G)]
        ident_raw = keep.tile([P, P], F32, name="ident_raw", align_bytes=64)
        ident = keep.tile([P, P], F32, name="ident", align_bytes=64)

        out_words = out_1[0].rearrange("p m t -> p (m t)")

        x_sorted, x_bank, x_turned, x_quant = {}, {}, {}, {}
        h_bank, h_bf16, h_quant_01, h_quant_2 = {}, {}, {}, {}
        d_bank, d_squared, y_f32, y_bf16 = {}, {}, {}, {}

        def live(i):
            return 0 <= i < TILES


        def load_x(i):
            g, n = divmod(i, TILES_PER_MOL)
            nc.sync.dma_start(out=x_raw[i][:], in_=dalpha[g, n * P:(n + 1) * P, :])

        def load_scales(tiles, src, runs, chunks, g):
            for r in range(4):
                nc.sync.dma_start(
                    out=tiles[g][r:P:QUADRANT, :, :].bitcast(I32),
                    in_=src[chunks * g:chunks * runs[g], r:16:4, :].rearrange("g q n -> q g n").bitcast(I32),
                )

        def load_j(tile, g, cols):
            nc.sync.dma_start(
                out=tile[:].bitcast(I32),
                in_=jac_words[K_CHUNKS * g:K_CHUNKS * (g + 1), :, cols].rearrange("g p n -> p g n").bitcast(I32),
            )

        def load_l(g):
            nc.sync.dma_start(
                out=l_words[g][:].bitcast(I32),
                in_=mode_words[F_CHUNKS * g:F_CHUNKS * (g + 1), :, :].rearrange("g p n -> p g n").bitcast(I32),
            )

        def load_row(tile, src, g):
            nc.sync.dma_start(out=tile[:], in_=src[g].partition_broadcast(P))

        def load_stage1_operands(g):
            if g in J_SCALE_RUNS:
                load_scales(j_scales, jac_scales, J_SCALE_RUNS, K_CHUNKS, g)
            load_j(j_later[g], g, slice(0, 2 * F))
            load_row(isq[g], isqm, g)

        def load_stage2_operands(g):
            if g in L_SCALE_RUNS:
                load_scales(l_scales, mode_scales, L_SCALE_RUNS, F_CHUNKS, g)
            load_l(g)
            load_row(oc[g], occ, g)
            load_row(vf[g], vfac, g)


        def new_bank(name):
            return psum.tile([P, 2, 2, P], F32, name=name, bufs=2 if name == "ps_d" else 1)

        def turn(bank, half, sorted_chunk):
            words = sorted_chunk[:].bitcast(F32)
            for u in range(2):
                nc.tensor.transpose(bank[:, half, u, :], words[:, u * P:(u + 1) * P], ident[:])

        def copy_out(dst, src, move=nc.scalar.copy):
            move(out=dst.bitcast(F32).rearrange("p c (r u) -> p c r u", u=2), in_=src.rearrange("p c u r -> p c r u"))

        def copy_halves(name, bank, lo, hi, move=nc.scalar.copy):
            dst = work.tile([P, 2, CHUNK], BF16, name=name, align_bytes=64)
            copy_out(dst[:, lo:hi, :], bank[:, lo:hi, :, :], move)
            return dst

        def quantize(name, src, chunks):
            codes = work.tile([P, chunks * P], U32, name=name + "_codes", align_bytes=64)
            scales = work.tile([P, chunks * P], U8, name=name + "_scales", align_bytes=64)
            nc.vector.quantize_mx(out=codes[:].bitcast(FP8X4), scales=scales[:], in_=src)
            return codes, scales


        def sort_x(i):
            xs = work.tile([P, K_CHUNKS, 2, P], F32, name="xs", align_bytes=64)
            nc.scalar.copy(out=xs[:], in_=x_raw[i][:].bitcast(F32).rearrange("r (c p u) -> r c u p", p=P, u=2))
            x_sorted[i] = xs

        def turn_x(i, name="ps_x"):
            bank = new_bank(name)
            words = x_raw[i][:].bitcast(F32).rearrange("r (c p u) -> r c u p", p=P, u=2)
            for c in range(K_CHUNKS):
                for u in range(2):
                    src = words[:, c, u, :] if i < UNSORTED_TILES else x_sorted[i][:, c, u, :]
                    nc.tensor.transpose(bank[:, c, u, :], src, ident[:])
            x_bank[i] = bank

        def copy_x(i):
            x_turned[i] = copy_halves("xg", x_bank[i], 0, K_CHUNKS)

        def quantize_x(i):
            x_quant[i] = quantize("xq", x_turned[i][:].rearrange("p c n -> p (c n)"), K_CHUNKS)


        def spread_isq(lo, hi, name):
            bank = new_bank(name)
            for j in range(lo, hi):
                words = isq_col[:, j, :].bitcast(F32)
                for u in range(2):
                    nc.tensor.transpose(bank[:, j - lo, u, :], words[:, u:u + 1].to_broadcast([P, P]), ident[:])
            return bank

        def copy_isq(lo, hi, bank):
            nc.vector.tensor_copy(
                out=isq[0][:, lo * CHUNK:hi * CHUNK].bitcast(F32).rearrange("r (j p u) -> r j p u", p=P, u=2),
                in_=bank[:, 0:hi - lo, :, :].rearrange("r j u p -> r j p u"),
            )


        def stage1(i):
            g = i // TILES_PER_MOL
            codes, scales = x_quant[i]
            for j in range(F_CHUNKS):
                bank = psum.tile([P, CHUNK], F32, name="ps_h%d" % j)
                for c in range(K_CHUNKS):
                    words = j_first[j][:, c, :] if g == 0 else j_later[g][:, c, 2 * CHUNK * j:2 * CHUNK * (j + 1)]
                    nc.tensor.matmul_mx(
                        out=bank[:],
                        lhsT=codes[:, c * P:(c + 1) * P].bitcast(FP8X4),
                        lhsT_scale=scales[:, c * P:(c + 1) * P],
                        rhs=words.bitcast(FP4X4),
                        rhs_scale=scale_plane(j_scales, K_CHUNKS, g, c)[:, j * CHUNK:(j + 1) * CHUNK],
                        start=(c == 0),
                        stop=(c == K_CHUNKS - 1),
                    )
                h_bank[i, j] = bank

        def weight_h(i):
            for j in range(F_CHUNKS):
                hb = work.tile([P, CHUNK], BF16, name="hb%d" % j, align_bytes=64)
                nc.vector.tensor_tensor(
                    out=hb[:].rearrange(SORTED, u=2, e=2),
                    in0=h_bank[i, j][:].rearrange(NATURAL, u=2, e=2),
                    in1=isq[i // TILES_PER_MOL][:, j * CHUNK:(j + 1) * CHUNK].rearrange(NATURAL, u=2, e=2),
                    op=ALU.mult,
                )
                h_bf16[i, j] = hb

        def stage2(i, name="ps_d"):
            g = i // TILES_PER_MOL
            bank = new_bank(name)[:].rearrange("r a b c -> r (a b c)")
            order = [0, 1, 2] if i == LAST else [2, 1, 0]
            for j in order:
                codes, scales = h_quant_01[i] if j < 2 else h_quant_2[i]
                cols = slice((j % 2) * P, (j % 2 + 1) * P)
                nc.tensor.matmul_mx(
                    out=bank,
                    lhsT=codes[:, cols].bitcast(FP8X4),
                    lhsT_scale=scales[:, cols],
                    rhs=l_words[g][:, j, :].bitcast(FP4X4),
                    rhs_scale=scale_plane(l_scales, F_CHUNKS, g, j),
                    start=(j == order[0]),
                    stop=(j == order[-1]),
                )
            d_bank[i] = bank

        def make_factor(g, cols):
            nc.vector.scalar_tensor_tensor(
                out=fac[g][:, cols], in0=oc[g][:, cols], scalar=1.0, in1=vf[g][:, cols], op0=ALU.add, op1=ALU.mult
            )

        def square(i):
            sq = work.tile([P, M], F32, name="sq", align_bytes=64)
            nc.scalar.activation(out=sq[:], in_=d_bank[i], func=ACT.Square)
            d_squared[i] = sq

        def finish_y(i):
            g, n = divmod(i, TILES_PER_MOL)
            y = work.tile([P, M], F32, name="y", align_bytes=64, bufs=6)
            nc.vector.tensor_tensor(out=y[:], in0=d_squared[i][:], in1=fac[g][:], op=ALU.mult)
            nc.sync.dma_start(out=out_0[g, n * P:(n + 1) * P, :], in_=y[:])
            y_f32[i] = y

        def round_y(i, move=nc.scalar.copy):
            yb = work.tile([P, M], BF16, name="yb", align_bytes=64)
            move(out=yb[:].rearrange(SORTED, u=2, e=2), in_=y_f32[i][:].rearrange(NATURAL, u=2, e=2))
            y_bf16[i] = yb

        def quantize_y(i, src):
            g, n = divmod(i, TILES_PER_MOL)
            nc.vector.quantize_mx(
                out=y_codes[g][:, n * P:(n + 1) * P].bitcast(FP8X4), scales=y_scales[g][:, n * P:(n + 1) * P], in_=src
            )

        def store_codes(g, lo, hi):
            nc.sync.dma_start(
                out=out_words[:, 4 * (R * g + lo):4 * (R * g + hi)].bitcast(I32), in_=y_codes[g][:, lo:hi].bitcast(I32)
            )

        def store_scales(g, queues):
            for q in range(4):
                queues[q].dma_start(
                    out=out_2[0, 4 * q:4 * q + 4, R * g:R * (g + 1)].bitcast(I32),
                    in_=y_scales[g][QUADRANT * q:QUADRANT * q + 4, :].bitcast(I32),
                )


        make_identity(nc, ident_raw[:])
        nc.scalar.activation(out=ident[:], in_=ident_raw[:], func=ACT.Square)
        for tile in (j_scales[0], l_scales[0], j_scales[1], l_scales[1], j_scales[2]):
            nc.vector.memset(tile[:].bitcast(I32), 0)
        load_x(0)
        nc.sync.dma_start(out=isq_col[:], in_=isqm[0].rearrange("(j p t) -> p j t", p=P, t=4))
        load_x(1)
        load_scales(j_scales, jac_scales, J_SCALE_RUNS, K_CHUNKS, 0)
        for j in range(F_CHUNKS):
            load_j(j_first[j], 0, slice(2 * CHUNK * j, 2 * CHUNK * (j + 1)))
        for i in range(2, LOAD_AHEAD):
            load_x(i)
        load_scales(l_scales, mode_scales, L_SCALE_RUNS, F_CHUNKS, 0)
        load_l(0)
        load_x(LOAD_AHEAD)
        load_row(oc[0], occ, 0)
        load_row(vf[0], vfac, 0)

        turn_x(0)
        isq_bank_01 = spread_isq(0, 2, "ps_ta")
        isq_bank_2 = spread_isq(2, 3, "ps_tb")
        copy_x(0)
        quantize_x(0)
        turn_x(1, "ps_d")
        copy_isq(0, 2, isq_bank_01)
        copy_isq(2, 3, isq_bank_2)
        copy_x(1)
        stage1(0)
        quantize_x(1)
        for i in range(UNSORTED_TILES, SORT_AHEAD):
            sort_x(i)
        turn_x(2, "ps_d")
        copy_x(2)
        sort_x(SORT_AHEAD)
        weight_h(0)
        quantize_x(2)


        for s in range(1, TILES):
            g, n = divmod(s, TILES_PER_MOL)
            x_tile, h_tile, e_tile, y_tile = s + TURN_AHEAD, s - 1, s - EPILOGUE_BEHIND, s - PLANES_BEHIND
            if live(s + LOAD_AHEAD):
                load_x(s + LOAD_AHEAD)
            if g + 1 < G and n == 1:
                load_stage1_operands(g + 1)
            if g + 1 < G and n == 3:
                load_stage2_operands(g + 1)

            bank_b = new_bank("ps_tb")
            if live(y_tile):
                turn(bank_b, 1, y_bf16[y_tile])
            if live(x_tile):
                turn_x(x_tile)
            chunk2_first = live(h_tile - STAGE2_BEHIND) and live(x_tile)
            if chunk2_first:
                turn(bank_b, 0, h_bf16[h_tile, 2])
            bank_a = new_bank("ps_ta")
            turn(bank_a, 0, h_bf16[h_tile, 0])
            turn(bank_a, 1, h_bf16[h_tile, 1])
            if not chunk2_first:
                turn(bank_b, 0, h_bf16[h_tile, 2])
            stage1(s)

            hx = work.tile([P, 2 + K_CHUNKS, CHUNK], BF16, name="hx", align_bytes=64)
            if live(e_tile):
                square(e_tile)
                finish_y(e_tile)
            if live(x_tile):
                copy_out(hx[:, 2:2 + K_CHUNKS, :], x_bank[x_tile][:])
            copy_out(hx[:, 0:2, :], bank_a[:])
            hy = copy_halves("hy", bank_b, 0, 2 if live(y_tile) else 1)
            if live(e_tile):
                round_y(e_tile)
            if live(s + SORT_AHEAD):
                sort_x(s + SORT_AHEAD)
            weight_h(s)
            chunks = 2 + K_CHUNKS if live(x_tile) else 2
            hx_codes = work.tile([P, (2 + K_CHUNKS) * P], U32, name="hx_codes", align_bytes=64, bufs=4)
            hx_scales = work.tile([P, (2 + K_CHUNKS) * P], U8, name="hx_scales", align_bytes=64, bufs=4)
            nc.vector.quantize_mx(
                out=hx_codes[:, 0:chunks * P].bitcast(FP8X4),
                scales=hx_scales[:, 0:chunks * P],
                in_=hx[:, 0:chunks, :].rearrange("p c n -> p (c n)"),
            )
            h_quant_01[h_tile] = (hx_codes[:, 0:2 * P], hx_scales[:, 0:2 * P])
            x_quant[x_tile] = (hx_codes[:, 2 * P:], hx_scales[:, 2 * P:])
            h_quant_2[h_tile] = quantize("h2", hy[:, 0, :], 1)
            if live(y_tile):
                quantize_y(y_tile, hy[:, 1, :])
                if y_tile % TILES_PER_MOL == TILES_PER_MOL - 1:
                    store_codes(y_tile // TILES_PER_MOL, 0, R)
                    store_scales(y_tile // TILES_PER_MOL, [nc.sync] * 4)
            if g == 0 and n == 2:
                make_factor(g, slice(0, M))
            if g > 0 and n in (1, 2):
                make_factor(g, slice((n - 1) * M // 2, n * M // 2))
            if live(s - STAGE2_BEHIND):
                stage2(s - STAGE2_BEHIND)


        bank_a = new_bank("ps_ta")
        turn(bank_a, 0, h_bf16[LAST, 0])
        turn(bank_a, 1, h_bf16[LAST, 1])
        bank_b = new_bank("ps_tb")
        turn(bank_b, 0, h_bf16[LAST, 2])
        turn(bank_b, 1, y_bf16[LAST - 3])
        square(LAST - 2)
        h01 = copy_halves("ha", bank_a, 0, 2)
        hy = copy_halves("hy", bank_b, 0, 2)
        finish_y(LAST - 2)
        h_quant_01[LAST] = quantize("h01", h01[:].rearrange("p c n -> p (c n)"), 2)
        round_y(LAST - 2, nc.vector.tensor_copy)
        stage2(LAST - 1, "ps_h0")
        square(LAST - 1)
        h_quant_2[LAST] = quantize("h2", hy[:, 0, :], 1)
        quantize_y(LAST - 3, hy[:, 1, :])
        stage2(LAST, "ps_h1")
        finish_y(LAST - 1)

        sq = work.tile([P, M], F32, name="sq", align_bytes=64)
        yb = work.tile([P, M], BF16, name="yb", align_bytes=64)
        for h in range(2):
            cols = slice(h * M // 2, (h + 1) * M // 2)
            nc.scalar.activation(out=sq[:, cols], in_=d_bank[LAST][:, cols], func=ACT.Square)
            nc.vector.tensor_tensor(
                out=yb[:].rearrange(SORTED, u=2, e=2)[:, :, h * P // 2:(h + 1) * P // 2, :],
                in0=sq[:, cols].rearrange(NATURAL, u=2, e=2),
                in1=fac[G - 1][:, cols].rearrange(NATURAL, u=2, e=2),
                op=ALU.mult,
            )
        d_squared[LAST] = sq
        y_bf16[LAST] = yb
        round_y(LAST - 1)

        y_banks = []
        for i, name in zip(range(LAST - 2, TILES), ["ps_ta", "ps_tb", "ps_h2"]):
            bank = new_bank(name)
            turn(bank, 0, y_bf16[i])
            y_banks.append(bank)
        y_turned_0 = copy_halves("ha", y_banks[0], 0, 1)
        y_turned_1 = copy_halves("hy", y_banks[1], 0, 1)
        finish_y(LAST)
        quantize_y(LAST - 2, y_turned_0[:, 0, :])
        y_turned_2 = copy_halves("ha", y_banks[2], 0, 1, nc.vector.tensor_copy)
        quantize_y(LAST - 1, y_turned_1[:, 0, :])
        store_codes(G - 1, 0, R - P)
        quantize_y(LAST, y_turned_2[:, 0, :])
        store_codes(G - 1, R - P, R)
        store_scales(G - 1, [nc.scalar, nc.scalar, nc.sync, nc.sync])
